import numpy as np, ml_dtypes
CORES = [25,29,65,69,153,157,193,197]
N = 8
BF = ml_dtypes.bfloat16
def gentries(a):
    return np.ascontiguousarray(a.reshape(8, 16, -1).transpose(0, 2, 1)).reshape(8, -1)
def gtable(e):
    e = np.asarray(e); return np.ascontiguousarray(e.reshape(8, -1, 16).transpose(0, 2, 1)).reshape(128, -1).astype(np.int32)
W, L, T, TH, A, B, FO = 2048, 128, 8, 58, 3, 9, 8
def parts(rng):
    return (rng.integers(0, 16, (N, 8, 16, W)), rng.integers(0, W, (N, 8, 16, W)), rng.integers(0, 64, (N, 8, 16, L)), rng.integers(0, W, (N, 8, 16, L)),
            rng.integers(0, W, (N, 8, 16, L)), rng.integers(0, 16, (N, 8, 16, L)), rng.integers(0, W, (N, 8, L)), rng.integers(0, 64, (N, 8, 16)))
def keys(x, w, p):
    z = np.take_along_axis(x, p[:, :, None, :], 3)
    return np.add.reduce(z * w[..., None], axis=2) & 63
def pack(x, d, m, u, n, q, o, w):
    return {"feat": np.ascontiguousarray(x.reshape(N, 128, W)).astype(np.float32).astype(BF), "kids": np.ascontiguousarray(d.reshape(N, 128, W)).astype(np.int32),
            "mkey": np.ascontiguousarray(m.reshape(N, 128, L)).astype(np.float32).astype(BF), "mobj": np.ascontiguousarray(u.reshape(N, 128, L)).astype(np.int32),
            "cand": np.stack([gtable(a.transpose(0, 2, 1).reshape(8, -1)) for a in n]), "want": np.ascontiguousarray(q.reshape(N, 128, L)).astype(np.float32).astype(BF),
            "last": np.ascontiguousarray(o).astype(np.int32), "wts": np.ascontiguousarray(w.reshape(N, 128, 1)).astype(np.int32)}
def setup_inputs(rng):
    return pack(*parts(rng))
def setup_inputs_corners(rng):
    x, d, m, u, n, q, o, w = parts(rng); own = np.arange(W)[None, None, None, :]
    kind = rng.integers(0, 7, (N, 8, 1, W))
    d = np.where(kind == 0, own, d); d = np.where(kind == 1, (own + 1) % W, d)
    d = np.where(kind == 2, (W - 1) * rng.integers(0, 2, d.shape), d); d = np.where(kind == 3, d[:, :, :1, :], d)
    d[2] = d[2] & -2
    x[3, :, 0] = (x[3, :, 0] & 14) | (own[0, 0] & 1); w[3] = w[3] & 62; w[3, :, 0] = w[3, :, 0] | 1
    p = rng.integers(0, W, (N, 8, L)); p[1] = 1 + np.argsort(rng.random((8, W - 2)), axis=1)[:, :L]
    p[:, :, 0] = 0; p[:, :, L - 1] = W - 1; p[3] = p[3] | 1
    n0 = n[0]; n = np.repeat(p[:, :, None, :], 16, axis=2); n[0] = np.where(rng.random((8, 1, L)) < 0.5, n0, n[0])
    j = rng.choice(np.array([0, A - 1, A, B - 1, B, 15, 16]), (N, 8, L))
    j[1] = np.where(j[1] == 16, 15, j[1]); j[2] = 16; j[3] = np.where(j[3] == 16, 0, j[3]); j[3, 7, L - 1] = 16
    c = keys(x, w, p)[:, :, None, :]; rows = np.arange(16)[None, None, :, None]; jj = j[:, :, None, :]
    off = rng.integers(1, 64, m.shape); off[3] = 2 * rng.integers(1, 32, off[3].shape)
    m = np.where((rows == jj) | ((rows > jj) & (rng.random(m.shape) < 0.2)), c, (c + off) & 63)
    m[1, :, :, 1] = c[1, :, :, 1]
    s = rng.integers(0, 5, u.shape); u = np.where(s == 0, 0, np.where(s == 1, W - 1, np.where(s == 2, p[:, :, None, :], u)))
    s = rng.integers(0, 4, o.shape); o = np.where(s == 0, 0, np.where(s == 1, W - 1, np.where(s == 2, p, o)))
    u[1, :, :, 1] = rng.integers(1, W - 1, (8, 16)); u[1, :, :, L - 1] = rng.integers(1, W - 1, (8, 16))
    z = np.take_along_axis(x[1], p[1][:, None, :], 2)
    q[1, 6] = z[6]; q[1, 7] = np.where(z[7] >= 8, 0, 15); u[1, 6, 0, 0] = W - 1; o[1, 6, 0] = 0
    return pack(x, d, m, u, n, q, o, w)
def setup_inputs_ends(rng):
    x, d, m, u, n, q, o, w = parts(rng)
    x = 15 * (rng.random((N, 8, 16, W)) < rng.choice(np.array([0.0, 0.3, 0.5, 0.5, 0.7, 1.0]), (N, 8, 1, W))).astype(np.int64)
    for g in range(8):
        x[:, g, :, 0] = 15 * (g & 1); x[:, g, :, W - 1] = 15 * (g & 1)
        x[:, g, :, W - 2] = 15 * (g & 1); x[:, g, 15, W - 2] = 15 - 15 * (g & 1)
    w = 63 * rng.integers(0, 2, w.shape); w[:, 6:] = 63; w[:, 0] = 0
    q = 15 * rng.integers(0, 2, q.shape)
    d = np.where(rng.random(d.shape) < 0.7, (W - 1) * rng.integers(0, 2, d.shape), d)
    n = np.where(rng.random(n.shape) < 0.7, (W - 1) * rng.integers(0, 2, n.shape), n)
    u = np.where(rng.random(u.shape) < 0.7, (W - 1) * rng.integers(0, 2, u.shape), u)
    o = np.where(rng.random(o.shape) < 0.75, (W - 1) * rng.integers(0, 2, o.shape), o)
    m = np.where(rng.random(m.shape) < 0.7, 63 * rng.integers(0, 2, m.shape), (49 * rng.integers(0, 17, m.shape)) & 63)
    for l in (0, 1, 2, 3, L - 4, L - 3, L - 2, L - 1): n[:, :, 0::2, l] = W - 1; n[:, :, 1::2, l] = 0
    for l, k in ((2, 1), (3, 13), (L - 4, 1), (L - 3, 13)): n[:, :, k, l] = W - 2; n[:, :, 14, l] = W - 2
    for g in range(8):
        for l in (1, 2, 3, L - 4, L - 3, L - 1): q[:, g, :, l] = 15 - 15 * (g & 1)
        for l in (0, L - 2): q[:, g, :, l] = 15 * (g & 1)
    kk = keys(x, w, np.full((N, 8, 1), W - 1))
    m[:, :, 12:, L - 1] = 63; u[:, :, 12:, L - 1] = W - 1
    m[:, :, 11, 1] = kk[:, :, 0]; m[:, :, 11, L - 1] = kk[:, :, 0]
    h = W // FO
    d[:, 7, 15, h - 1::h] = W - 1; d[:, 7, 15, h - 2::h] = W - 1; d[:, :, 0, 0::h] = 0
    return pack(x, d, m, u, n, q, o, w)
def setup_inputs_shared(rng):
    x, d, m, u, n, q, o, w = parts(rng)
    hot = np.stack([np.concatenate([np.array([0, W - 1]), 1 + rng.permutation(W - 2)[:22]]) for g in range(8)])
    gg = np.arange(8)[None, :, None, None]
    d = hot[gg, rng.integers(0, 24, d.shape)]; n = hot[gg, rng.integers(0, 24, n.shape)]
    u = np.where(rng.random(u.shape) < 0.5, hot[gg, rng.integers(0, 24, u.shape)], u)
    kh = keys(x, w, np.repeat(hot[None], N, axis=0))
    m = np.where(rng.random(m.shape) < 0.6, kh[np.arange(N)[:, None, None, None], gg, rng.integers(0, 24, m.shape)], m)
    for r, g, i in ((0, 0, 2), (N - 1, 7, 1)):
        n[r, g] = hot[g, i]; m[r, g, 0] = kh[r, g, i]; u[r, g, 0, 0] = hot[g, 3]
    return pack(x, d, m, u, n, q, o, w)
def setup_inputs_spread(rng):
    x, d, m, u, n, q, o, w = parts(rng)
    def uneven(top, shape, kshape):
        return np.minimum((top * rng.random(shape) ** np.exp2(rng.integers(-2, 3, kshape))).astype(np.int64), top - 1)
    x = uneven(16, x.shape, (N, 8, 1, W)); q = uneven(16, q.shape, (N, 8, 1, L)); d = uneven(W, d.shape, (N, 8, 16, 1))
    u = uneven(W, u.shape, (N, 8, 1, L)); n = uneven(W, n.shape, (N, 8, 16, 1)); o = uneven(W, o.shape, (N, 8, 1)); w = uneven(64, w.shape, (N, 8, 1))
    m = m & rng.choice(np.array([63, 63, 7, 56, 1]), (N, 8, 1, L))
    return pack(x, d, m, u, n, q, o, w)
def setup_inputs_ties(rng):
    x, d, m, u, n, q, o, w = parts(rng); h = W // 2
    x[..., h:] = x[..., :h][..., ::-1]
    p = rng.integers(0, W, (N, 8, L)); p[:, :, L - 1] = W - 1
    z = np.take_along_axis(x, p[:, :, None, :], 3); tot = TH + rng.integers(-1, 2, (N, 8, 1, L))
    dl = (tot >> 4) + (np.arange(16)[None, None, :, None] < (tot & 15))
    q = np.where(z >= 8, z - dl, z + dl)
    twin = np.where(rng.random(n.shape) < 0.5, p[:, :, None, :], W - 1 - p[:, :, None, :])
    n = np.where(rng.random(n.shape) < 0.6, twin, n)
    c = keys(x, w, p)[:, :, None, :]
    m = np.where(rng.random((N, 8, 1, L)) < 0.4, (c + (m & 3)) & 63, m)
    return pack(x, d, m, u, n, q, o, w)
def check_inputs(d):
    bad = []
    for k, lo, hi in (("feat", 0, 15), ("kids", 0, W - 1), ("mkey", 0, 63), ("mobj", 0, W - 1), ("cand", 0, W - 1), ("want", 0, 15), ("last", 0, W - 1), ("wts", 0, 63)):
        v = np.asarray(d[k]).astype(np.float64)
        if not (np.min(v) >= lo and np.max(v) <= hi and np.all(v == np.rint(v))): bad.append("range of " + k)
    return bad
def reference(feat, kids, mkey, mobj, cand, want, last, wts):
    x = np.ascontiguousarray(feat.astype(np.int32).reshape(N, 8, 16, W).transpose(0, 1, 3, 2))
    d = np.array(kids.astype(np.int64).reshape(N, 8, 16, W).transpose(0, 1, 3, 2))
    m = np.array(mkey.astype(np.int64).reshape(N, 8, 16, L).transpose(0, 1, 3, 2))
    u = np.array(mobj.astype(np.int64).reshape(N, 8, 16, L).transpose(0, 1, 3, 2))
    n = np.stack([gentries(a) for a in cand]).astype(np.int64).reshape(N, 8, L, 16)
    q = np.array(want.astype(np.int32).reshape(N, 8, 16, L).transpose(0, 1, 3, 2))
    prev = np.array(last.astype(np.int64)); w = wts.astype(np.int64).reshape(N, 8, 1, 16)
    count = np.zeros(N, np.int64); gi = np.arange(8)[:, None]
    for t in range(T):
        seen = np.zeros(N, np.int64)
        for r in range(N):
            s = (r + t) % N
            dist = np.add.reduce(np.abs(x[s][gi[:, :, None], n[r]] - q[r][:, :, None, :]), axis=3)
            like = dist < TH + (count[s] & 15); alike = np.any(like, axis=2)
            k = np.where(alike, np.argmax(like, axis=2), np.argmin(dist, axis=2))
            o = np.take_along_axis(n[r], k[:, :, None], 2)[:, :, 0]
            xo = x[s][gi, o]; c = np.add.reduce(xo * w[s], axis=2) & 63
            hit = m[s] == c[:, :, None]; covered = np.any(hit, axis=2); j = np.argmax(hit, axis=2)
            own = d[s][gi, o]; e = d[s][gi, np.take_along_axis(u[s], j[:, :, None], 2)[:, :, 0]]
            top = covered & (j < B); low = covered & ((j < A) | (j >= B))
            new = np.concatenate([np.where(top[:, :, None], e[:, :, :8], own[:, :, :8]), np.where(low[:, :, None], e[:, :, 8:], own[:, :, 8:])], axis=2)
            g, l = np.nonzero(covered); first = np.unique(g * W + o[g, l], return_index=True)[1]
            g, l = g[first], l[first]; d[s, g, o[g, l]] = new[g, l]
            g, l = np.nonzero(~alike); row = (l + 5 * t) & 15
            m[s, g, l, row] = c[g, l]; u[s, g, l, row] = prev[r, g, l]
            seen[s] = np.count_nonzero(covered); prev[r] = o; n[r] = new; q[r] = np.abs(q[r] - xo)
        count = seen
    dd = d.transpose(0, 1, 3, 2).reshape(N, 128, FO, W // FO)
    return {"yn": n.transpose(0, 1, 3, 2).reshape(N, 128, L).astype(np.float32), "ymu": (64 * u + m).transpose(0, 1, 3, 2).reshape(N, 128, L).astype(np.float32),
            "yd": np.add.reduce(dd * np.arange(1, FO + 1)[:, None], axis=2).astype(np.float32)}

@@ -1,0 +1,633 @@
+from concourse.mybir import AluOpType, AxisListType, ActivationFunctionType
+
+A = AluOpType
+AF = ActivationFunctionType
+N, STEPS, L, W = 8, 8, 128, 2048
+H = 2
+LH = L // H
+C = LH // 16
+NCH = LH // 32
+D0 = 128
+KW = D0 + W
+BIG = 16777216.0
+RND = 12582912.0
+S_GATHER = {1: (0,), 2: (0,)}[H]
+TRANSIT = 5.0
+
+SCRATCH = {
+    "F": ("sbuf", [128, W], "bfloat16"), "KI": ("sbuf", [128, W], "int32"), "K": ("sbuf", [128, KW], "float32"),
+    "KT": ("sbuf", [128, W], "bfloat16"), "IDT": ("sbuf", [128, W], "float32"), "HI": ("sbuf", [128, W], "bfloat16"),
+    "CI": ("sbuf", [128, L], "int32"), "LI": ("sbuf", [128, L], "int32"), "LF": ("sbuf", [128, L], "float32"),
+    "MKB": ("sbuf", [128, L], "bfloat16"), "MOI": ("sbuf", [128, L], "int32"),
+    "WI": ("sbuf", [128, 1], "int32"), "CST": ("sbuf", [128, 512], "bfloat16"),
+    "IM": ("sbuf", [128, 128], "float32"), "RI": ("sbuf", [128, 128], "float32"), "GI": ("sbuf", [128, 128], "float32"),
+    "PC": ("sbuf", [128, 8], "int32"), "PA": ("sbuf", [128, 8], "int32"), "PB": ("sbuf", [128, 8], "int32"),
+    "PT": ("sbuf", [128, 8], "float32"), "CO": ("sbuf", [128, 32], "float32"), "P2": ("sbuf", [128, 48], "float32"),
+    "IF": ("sbuf", [128, 128], "float32"), "IB": ("sbuf", [128, 128], "bfloat16"), "NI": ("sbuf", [128, 128], "bfloat16"),
+    "N64": ("sbuf", [128, 128], "bfloat16"), "BF": ("sbuf", [128, 128], "float32"), "RB": ("sbuf", [128, 128], "bfloat16"),
+    "RF": ("sbuf", [128, 128], "float32"), "WA": ("sbuf", [128, 128], "bfloat16"), "WC": ("sbuf", [128, 128], "bfloat16"),
+    "B8": ("sbuf", [128, 128], "float32"),
+    "LR": ("sbuf", [128, 16, 128], "bfloat16"), "PI": ("sbuf", [128, 8, 128], "bfloat16"),
+    "PW": ("sbuf", [128, 8, 16], "bfloat16"), "PS_": ("sbuf", [128, 8, 16], "bfloat16"), "B3": ("sbuf", [128, 8, 16], "float32"),
+    "OD": ("sbuf", [128, LH], "bfloat16"), "NT": ("sbuf", [128, LH], "bfloat16"), "DG": ("sbuf", [128, LH], "float32"),
+    "R2": ("sbuf", [128, LH], "float32"), "SWM": ("sbuf", [128, 4, 128], "float32"),
+    "ON": ("sbuf", [128, 128], "float32"), "EXI": ("sbuf", [128, C], "int32"), "EX": ("sbuf", [128, C], "uint16"),
+    "ER": ("sbuf", [128, 16 * LH], "bfloat16"), "YI": ("sbuf", [128, 8, 128], "float32"),
+    "CN": ("sbuf", [128, 32], "float32"), "CC": ("sbuf", [128, 16], "int32"), "CA": ("sbuf", [128, 16], "int32"),
+    "LM": ("sbuf", [128, 16], "float32"),
+    "YN": ("sbuf", [128, L], "float32"), "YM": ("sbuf", [128, L], "float32"), "YD": ("sbuf", [128, 256], "float32"),
+    "YS": ("sbuf", [128, 4, 256], "float32"),
+    "X0": ("psum", [128, 2, 256], "float32"), "X1": ("psum", [128, 2, 256], "float32"),
+    "X2": ("psum", [128, 2, 256], "float32"), "QU": ("psum", [128, 512], "float32"),
+    "RYX": ("sbuf", [128, 7 * L], "bfloat16"), "RYN": ("sbuf", [128, 8 * 2 * L], "uint16"),
+}
+for _h in range(H):
+    SCRATCH["QD%d" % _h] = ("psum", [128, 32, 16], "float32")
+    SCRATCH["QC%d" % _h] = ("psum", [128, 512], "float32")
+    for _n, _s, _d in (("RN", [128, 18 * LH], "uint16"), ("RX", [128, 8 * LH], "bfloat16"), ("TN", [128, 16 * LH], "uint16"),
+                       ("TX", [128, 8 * LH], "bfloat16"), ("TL", [128, LH], "float32"), ("CL", [128, 2 * LH], "float32"),
+                       ("MM", [128, 2 * LH], "float32"), ("QT", [128, 128], "bfloat16"),
+                       ("NF", [128, LH], "float32"), ("XT", [128, NCH, 32], "float32"), ("Z", [128, 16 * LH], "bfloat16"),
+                       ("AX", [128, C, 256], "bfloat16"), ("S1", [128, C, 16], "float32"), ("S2", [128, LH], "float32"),
+                       ("SC", [128, LH], "int32"), ("OI", [128, C], "int32"), ("OL", [128, C], "uint16"), ("HT", [128, LH], "bfloat16"),
+                       ("SM", [128, 12 * LH], "float32"), ("SB", [128, LH], "bfloat16"), ("LT", [128, 40], "float32"),
+                       ("EL", [128, C], "uint16"), ("SL", [128, 2 * C], "uint16"), ("ND", [128, LH], "bfloat16"),
+                       ("DD", [128, 2 * LH], "float32")):
+        SCRATCH[_n + str(_h)] = ("sbuf", _s, _d)
+
+DMAS = ["cand", "feat"] + ["want%d" % _h for _h in range(H)] + ["wts", "last", "mkey", "mobj", "kids", "oyn", "oym", "oyd"]
+SEMAPHORES = ["v", "a", "t", "gq", "ls"] + ["d_" + n for n in DMAS] + \
+    ["%s%d_%d" % (p, t, h) for p in ("ax", "an") for t in range(1, STEPS + (p == "an")) for h in range(H)]
+
+CTR = {"v": "v", "a": "a", "t": "t", "g": "gq"}
+PM, PWC, THR, KCC, SG1, SG2, PF, PG, B4, TG = 0, 1, 2, 3, 4, 5, 6, 7, 8, 9
+
+
+def build():
+    nodes = []
+
+    def op(q, us, R, Wr, fn, tag=None):
+        nodes.append((q, us, list(R), list(Wr), fn, tag))
+
+    def v(n, R, Wr, fn):
+        op("v", 0.03 + max(64, n) * 0.00104, R, Wr, fn)
+
+    def a(n, R, Wr, fn):
+        op("a", 0.06 + max(64, n) * 0.00104, R, Wr, fn)
+
+    def t_(cyc, R, Wr, fn):
+        op("t", 0.03 + cyc * 0.0007, R, Wr, fn)
+
+    def gq(n, Wr, fn):
+        op("g", 0.15 + n * 0.0017, [], Wr, fn)
+
+    def dma(q, name, R, Wr, out, in_, us=3.0):
+        op(q, us, R, Wr, lambda E: (E["g"].sync if q == "dy" else E["g"].scalar).dma_start(out(E["T"]), in_(E["T"])), "d_" + name)
+
+    dma("dy", "cand", [], ["CI"], lambda T: T.CI[:], lambda T: T.cand[:], 2.5)
+    dma("ds", "wts", [], ["WI"], lambda T: T.WI[:], lambda T: T.wts[:], 2.5)
+    dma("dy", "feat", [], ["F"], lambda T: T.F[:], lambda T: T.feat[:], 5.0)
+    for h in range(H):
+        dma("ds", "want%d" % h, [], [("RXq", h, 0)], lambda T, h=h: T["RX%d" % h][:, 0:LH], lambda T, h=h: T.want[:, h * LH:(h + 1) * LH], 3.0)
+    dma("dy", "last", [], ["LI"], lambda T: T.LI[0:8, :], lambda T: T.last[:], 5.5)
+    dma("ds", "mkey", [], ["MKB"], lambda T: T.MKB[:], lambda T: T.mkey[:], 5.5)
+    dma("dy", "mobj", [], ["MOI"], lambda T: T.MOI[:], lambda T: T.mobj[:], 6.0)
+    dma("ds", "kids", [], ["KI"], lambda T: T.KI[:], lambda T: T.kids[:], 8.0)
+
+    gq(8, ["PC"], lambda E: E["g"].iota(E["T"].PC[:], [[5, 8]], 0, 1))
+    gq(128, ["IM"], lambda E: E["g"].iota(E["T"].IM[:], [[1, 128]], 0, 0, allow_small_or_imprecise_dtypes=True))
+    gq(128, ["RI"], lambda E: E["g"].iota(E["T"].RI[:], [[0, 8], [1, 16]], 0, 0, allow_small_or_imprecise_dtypes=True))
+    gq(128, ["GI"], lambda E: E["g"].iota(E["T"].GI[:], [[1, 8], [0, 16]], 0, 0, allow_small_or_imprecise_dtypes=True))
+    gq(C, ["EXI"], lambda E: E["g"].iota(E["T"].EXI[:], [[1, C]], 0, 0))
+    gq(W, ["IDT"], lambda E: E["g"].iota(E["T"].IDT[:], [[1, W]], D0, 0, allow_small_or_imprecise_dtypes=True))
+
+    def ts(n, R, Wr, out, in0, s1, s2, o0, o1=None):
+        if o1 is None:
+            v(n, R, Wr, lambda E: E["g"].vector.tensor_scalar(out(E["T"]), in0(E["T"]), s1(E["T"]) if callable_(s1) else s1, None, o0))
+        else:
+            v(n, R, Wr, lambda E: E["g"].vector.tensor_scalar(out(E["T"]), in0(E["T"]), s1(E["T"]) if callable_(s1) else s1,
+                                                              s2(E["T"]) if callable_(s2) else s2, o0, o1))
+
+    def callable_(x):
+        return not isinstance(x, (int, float))
+
+    def tt(n, R, Wr, out, in0, in1, o, ind=False):
+        v(n * 2 if not ind else int(n * 2), R, Wr, lambda E: E["g"].vector.tensor_tensor(out(E["T"]), in0(E["T"]), in1(E["T"]), o))
+
+    def tc(n, R, Wr, out, in_):
+        v(n, R, Wr, lambda E: E["g"].vector.tensor_copy(out(E["T"]), in_(E["T"])))
+
+    def ms(n, Wr, out, x):
+        v(n, [], Wr, lambda E: E["g"].vector.memset(out(E["T"]), x))
+
+    def act(n, R, Wr, out, in_, f=AF.Copy, scale=1.0):
+        a(n, R, Wr, lambda E: E["g"].scalar.activation(out(E["T"]), in_(E["T"]), f, scale=scale))
+
+    def mm(cyc, R, Wr, calls):
+        def emit(E):
+            i = None
+            for out, l, r, st, sp in calls:
+                i = E["g"].tensor.matmul(out(E["T"]), l(E["T"]), r(E["T"]), st, sp)
+            return i
+        t_(cyc, R, Wr, emit)
+
+    def co(i):
+        return lambda T: T.CO[:, i:i + 1]
+
+    def cpy(i):
+        return "co%d" % i
+
+    for h in range(H):
+        tc(LH, ["CI"], [("RN", h, 0), ("RNl", h, 0)], lambda T, h=h: T["RN%d" % h][:, 0:LH], lambda T, h=h: T.CI[:, h * LH:(h + 1) * LH])
+    ts(8, ["PC"], ["PA"], lambda T: T.PA[:], lambda T: T.PC[:], 15, None, A.bitwise_and)
+    tc(8, ["PA"], ["PT"], lambda T: T.PT[:], lambda T: T.PA[:])
+    tc(1, ["PC"], [cpy(PF)], co(PF), lambda T: T.PC[:, 0:1])
+    ts(1, ["PC"], ["PB0"], lambda T: T.PB[:, 0:1], lambda T: T.PC[:, 0:1], 4, None, A.arith_shift_right)
+    tc(1, ["PB0"], [cpy(PG)], co(PG), lambda T: T.PB[:, 0:1])
+    ts(1, ["PB0"], ["PB1"], lambda T: T.PB[:, 1:2], lambda T: T.PB[:, 0:1], 1, None, A.bitwise_and)
+    tc(1, ["PB1"], [cpy(B4)], co(B4), lambda T: T.PB[:, 1:2])
+    pm = lambda T: T.PT[:, 0:1]
+    ts(128, ["IM", cpy(PF)], ["IF"], lambda T: T.IF[:], lambda T: T.IM[:], co(PF), None, A.is_equal)
+    ts(128, ["IM", cpy(PF)], ["NI"], lambda T: T.NI[:], lambda T: T.IM[:], co(PF), -1.0, A.is_equal, A.mult)
+    ts(128, ["IM", cpy(PF)], ["IB"], lambda T: T.IB[:], lambda T: T.IM[:], co(PF), None, A.is_equal)
+    ts(128, ["GI", cpy(PG)], ["BF"], lambda T: T.BF[:], lambda T: T.GI[:], co(PG), None, A.is_equal)
+    for k in range(16):
+        tc(LH, ["IB"], [("ER", k)], lambda T, k=k: T.ER[:, k:16 * LH:16], lambda T: T.IB[:, 0:LH])
+    ERall = [("ER", k) for k in range(16)]
+    ts(128, ["GI", cpy(PG)], ["RF"], lambda T: T.RF[:], lambda T: T.GI[:], co(PG), 100.0, A.not_equal, A.mult)
+    tt(128, ["RF", "RI"], ["RB"], lambda T: T.RB[:], lambda T: T.RF[:], lambda T: T.RI[:], A.add)
+    for r in range(16):
+        ts(64, ["RB"], [("LR", r)], lambda T, r=r: T.LR[:, r, :], lambda T: T.RB[:], float(r), 32768.0, A.is_equal, A.mult)
+    LRall = [("LR", r) for r in range(16)]
+    tc(1, ["WI"], [cpy(16)], co(16), lambda T: T.WI[:])
+    ts(128, ["BF", cpy(16)], ["WA"], lambda T: T.WA[:], lambda T: T.BF[:], co(16), 1.0 / 64, A.mult, A.mult)
+    ts(128, ["BF", cpy(16)], ["WC"], lambda T: T.WC[:], lambda T: T.BF[:], co(16), None, A.mult)
+    ts(128, ["IF"], ["N64"], lambda T: T.N64[:], lambda T: T.IF[:], -64.0, None, A.mult)
+    ms(256, ["CST"], lambda T: T.CST[:], -63.0 / 128)
+
+    def keytable(b):
+        sl = slice(512 * b, 512 * b + 512)
+        XB = "X%d" % ((b + 1) % 3)
+        mm(1024, ["WA", "F", "IB", "CST"], [("bank", XB)], [
+            (lambda T, j=j: T[XB][:, j, :], lambda T: T.IB[:], lambda T, j=j: T.CST[:, 256 * j:256 * j + 256], True, False) if s == 0 else
+            (lambda T, j=j: T[XB][:, j, :], lambda T: T.WA[:], lambda T, j=j: T.F[:, 512 * b + 256 * j:512 * b + 256 * j + 256], False, True)
+            for j in range(2) for s in range(2)])
+        for j in range(2):
+            ts(256, [("bank", XB)], [("HI", b, j)], lambda T, j=j: T.HI[:, 512 * b + 256 * j:512 * b + 256 * j + 256],
+               lambda T, j=j: T[XB][:, j, :], RND, RND, A.add, A.subtract)
+        mm(1024, ["WC", "F", "N64", ("HI", b, 0), ("HI", b, 1)], [("bank", XB)], [
+            (lambda T, j=j: T[XB][:, j, :], lambda T: T.WC[:], lambda T, j=j: T.F[:, 512 * b + 256 * j:512 * b + 256 * j + 256], True, False) if s == 0 else
+            (lambda T, j=j: T[XB][:, j, :], lambda T: T.N64[:], lambda T, j=j: T.HI[:, 512 * b + 256 * j:512 * b + 256 * j + 256], False, True)
+            for j in range(2) for s in range(2)])
+        for j in range(2):
+            act(256, [("bank", XB)], [("KT", b, j)], lambda T, j=j: T.KT[:, 512 * b + 256 * j:512 * b + 256 * j + 256], lambda T, j=j: T[XB][:, j, :])
+    KTall = [("KT", b, j) for b in range(4) for j in range(2)]
+
+    def setup_rest():
+        ms(1, ["P2a"], lambda T: T.P2[:, 0:16], 0.5)
+        ms(1, ["P2b"], lambda T: T.P2[:, 16:32], 0.0)
+        v(16, ["P2a", "P2b"], ["P2c"], lambda E: E["g"].vector.tensor_tensor_scan(
+            E["T"].P2[:, 32:48], E["T"].P2[:, 0:16], E["T"].P2[:, 16:32], 65536.0, A.mult, A.add))
+        ts(64, ["RI", "PT"], ["DG"], lambda T: T.DG[:], lambda T: T.RI[:, 0:LH], pm, None, A.is_equal)
+        tt(16, ["P2c", "DG"], ["P2a"], lambda T: T.P2[:, 0:16], lambda T: T.P2[:, 32:48], lambda T: T.DG[:, 0:16], A.mult)
+        v(16, ["P2a"], [cpy(PWC)], lambda E: E["g"].vector.tensor_reduce(
+            E["T"].CO[:, PWC:PWC + 1], E["T"].P2[:, 0:16], AxisListType.X, A.add))
+        ts(1, [cpy(PWC)], [cpy(THR)], co(THR), co(PWC), 2.0, None, A.mult)
+        ts(1, ["PT"], [cpy(KCC)], co(KCC), pm, 2048.0, None, A.mult)
+        ts(1, ["PT"], [cpy(17)], co(17), pm, 9.0, -2.0, A.is_ge, A.mult)
+        ts(1, ["PT"], [cpy(18)], co(18), pm, 3.0, -2.0, A.is_ge, A.mult)
+        ts(1, [cpy(17)], [cpy(19)], co(19), co(17), 1.0, None, A.add)
+        tt(1, [cpy(18), cpy(17)], [cpy(20)], co(20), co(18), co(17), A.subtract)
+        ts(1, [cpy(20)], [cpy(22)], co(22), co(20), 1.0, None, A.add)
+        v(1, [cpy(19), cpy(PWC)], [cpy(SG1)], lambda E: E["g"].vector.tensor_tensor(E["T"].CO[:, SG1:SG1 + 1], E["T"].CO[:, 19:20], E["T"].CO[:, PWC:PWC + 1], A.mult))
+        v(1, [cpy(22), cpy(PWC)], [cpy(SG2)], lambda E: E["g"].vector.tensor_tensor(E["T"].CO[:, SG2:SG2 + 1], E["T"].CO[:, 22:23], E["T"].CO[:, PWC:PWC + 1], A.mult))
+        for g8 in range(8):
+            tc(16, ["BF"], [("B3", g8)], lambda T, g8=g8: T.B3[:, g8, :], lambda T, g8=g8: T.BF[:, 16 * g8:16 * g8 + 16])
+        B3 = [("B3", g8) for g8 in range(8)]
+        ts(128, B3 + [cpy(PWC)], ["PW"], lambda T: T.PW[:], lambda T: T.B3[:], co(PWC), None, A.mult)
+        ts(64, B3 + [cpy(SG1)], ["PSa"], lambda T: T.PS_[:, :, 0:8], lambda T: T.B3[:, :, 0:8], co(SG1), None, A.mult)
+        ts(64, B3 + [cpy(SG2)], ["PSb"], lambda T: T.PS_[:, :, 8:16], lambda T: T.B3[:, :, 8:16], co(SG2), None, A.mult)
+        ts(64, ["RI", "PT"], ["OD"], lambda T: T.OD[:], lambda T: T.RI[:, 0:LH], pm, 8192.0, A.not_equal, A.mult)
+        ts(64, ["RI", "PT"], ["NT"], lambda T: T.NT[:], lambda T: T.RI[:, 0:LH], pm, -131072.0, A.is_ge, A.mult)
+        tc(C, ["EXI"], ["EX"], lambda T: T.EX[:], lambda T: T.EXI[:])
+        ts(64, ["RI"], ["R2"], lambda T: T.R2[:], lambda T: T.RI[:, 0:LH], 0.0, BIG, A.is_equal, A.mult)
+        for g2 in range(2):
+            for c2 in range(2):
+                i = 2 * g2 + c2
+                ts(1, [cpy(PF)], [cpy(23 + i)], co(23 + i), co(PF), float(16 * (g2 - c2) + 1), None, A.add)
+                ts(1, [cpy(B4)], [cpy(27 + i)], co(27 + i), co(B4), float(c2), None, A.is_equal)
+                tt(1, [cpy(23 + i), cpy(27 + i)], [cpy(TG + i)], co(TG + i), co(23 + i), co(27 + i), A.mult)
+                ts(1, [cpy(TG + i)], [("tg", i)], co(TG + i), co(TG + i), -1.0, None, A.add)
+                ts(128, [("tg", i), "IM"], [("SWM", i)], lambda T, i=i: T.SWM[:, i, :], lambda T: T.IM[:], co(TG + i), None, A.is_equal)
+
+    def setup_late():
+        for h in range(H):
+            tc(LH, ["MKB"], [("MK", h)], lambda T, h=h: T["MM%d" % h][:, 0:LH], lambda T, h=h: T.MKB[:, h * LH:(h + 1) * LH])
+            ts(LH, ["MOI"], [("MO", h)], lambda T, h=h: T["MM%d" % h][:, LH:2 * LH], lambda T, h=h: T.MOI[:, h * LH:(h + 1) * LH], float(D0), None, A.add)
+        ms(128, ["Kd"], lambda T: T.K[:, 0:D0], 0.0)
+        for b in range(4):
+            tc(512, ["KI"], [("Kb", b)], lambda T, b=b: T.K[:, D0 + 512 * b:D0 + 512 * b + 512], lambda T, b=b: T.KI[:, 512 * b:512 * b + 512])
+        for t in range(8):
+            ts(128, ["RB", "PT"], [("PI", t)], lambda T, t=t: T.PI[:, t, :], lambda T: T.RB[:], lambda T, t=t: T.PT[:, t:t + 1], None, A.is_equal)
+        ms(128, ["ON"], lambda T: T.ON[:], 1.0 / 16)
+        tc(128, ["LI"], ["LF"], lambda T: T.LF[0:8, :], lambda T: T.LI[0:8, :])
+        ts(128, ["GI", cpy(PF)], ["B8"], lambda T: T.B8[:], lambda T: T.GI[:], co(PF), None, A.is_equal)
+        mm(512, ["B8", "LF"], [("bank", "QU")], [(lambda T: T.QU[:, 0:128], lambda T: T.B8[0:8, :], lambda T: T.LF[0:8, :], True, True)])
+        for h in range(H):
+            ts(LH, [("bank", "QU")], [("CLl", h)], lambda T, h=h: T["CL%d" % h][:, LH:2 * LH], lambda T, h=h: T.QU[:, h * LH:(h + 1) * LH], float(D0), None, A.add)
+        for b in range(8):
+            ts(128, ["IF"], [("YI", b)], lambda T, b=b: T.YI[:, b, :], lambda T: T.IF[:], float(b + 1), None, A.mult)
+
+    ms(1, ["LM0"], lambda T: T.LM[:, 0:1], 57.0 * 32768)
+    ms(1, ["LI0"], lambda T: T.LM[:, 8:9], 58.0 * 32768)
+    Kall = ["Kd"] + [("Kb", b) for b in range(4)] + ["K"]
+
+    def front(t, h):
+        RN, RX = "RN%d" % h, "RX%d" % h
+        QC, QD = "QC%d" % h, "QD%d" % h
+        mm(128, [("RXq", h, t), "IB"], [("bank", QC), ("qt", h)], [
+            (lambda T: T[QC][0:LH, 384:512], lambda T: T[RX][:, LH * t:LH * t + LH], lambda T: T.IB[:], True, True)])
+        act(128, [("bank", QC), ("qt", h)], [("QT", h)], lambda T: T["QT%d" % h][0:LH, :], lambda T: T[QC][0:LH, 384:512])
+        ts(LH, [("RN", h, t), cpy(KCC)], [("NF", h)], lambda T: T["NF%d" % h][:], lambda T: T[RN][:, 2 * LH * t:2 * LH * t + LH], co(KCC), None, A.add)
+
+        def turn(E):
+            i = None
+            for b in range(NCH):
+                i = E["g"].vector.transpose(E["T"]["XT%d" % h][:, b, :], E["T"]["NF%d" % h][:, 32 * b:32 * b + 32])
+            return i
+        v(64 * NCH, [("NF", h)], [("XT", h)], turn)
+        for m in range(NCH):
+            zs = slice(512 * m, 512 * m + 512)
+            XB = "X%d" % ((h * NCH + m) % 3)
+            for j in range(2):
+                cols = slice(2 * LH * t + 32 * m + 16 * j, 2 * LH * t + 32 * m + 16 * j + 16)
+                z2 = slice(512 * m + 256 * j, 512 * m + 256 * j + 256)
+                if m in S_GATHER:
+                    a(256 * 1.5 + 60, ["F", ("RN", h, t)], [("Z", h, m, j)], lambda E, zs=z2, cols=cols: E["g"].scalar.activation(
+                        E["T"]["Z%d" % h][:, zs], E["T"].F[:, 0:W].indirect(E["T"][RN][:, cols]), AF.Copy))
+                else:
+                    v(256 * 1.5 + 50, ["F", ("XT", h), ("RN", h, t)], [("Z", h, m, j)], lambda E, zs=z2, cols=cols: E["g"].vector.tensor_copy(
+                        E["T"]["Z%d" % h][:, zs], E["T"].F[:, 0:W].indirect(E["T"][RN][:, cols])))
+            mm(512, [("QT", h)] + ERall, [("bank", XB), ("xq", h, m)], [
+                (lambda T, XB=XB: T[XB][:], lambda T: T["QT%d" % h][0:LH, :], lambda T, zs=zs: T.ER[0:LH, zs], True, False)])
+            mm(512, ["NI", ("Z", h, m, 0), ("Z", h, m, 1), ("xq", h, m)], [("bank", XB), ("xd", h, m)], [
+                (lambda T, XB=XB: T[XB][:], lambda T: T.NI[:], lambda T, zs=zs: T["Z%d" % h][:, zs], False, True)])
+            act(512, [("bank", XB), ("xd", h, m)], [("AX", h, m)], lambda T, m=m: T["AX%d" % h][:, 2 * m:2 * m + 2, :], lambda T, XB=XB: T[XB][:], AF.Abs)
+        for c2 in range(2):
+            mm(512, [("XT", h)] + [("SWM", i) for i in range(4)], [("bank", QD), ("KN", h, c2)], [
+                (lambda T, c2=c2: T[QD][:, 16 + c2:16 + C:2, :], lambda T, g2=g2, c2=c2: T.SWM[:, 2 * g2 + c2, :],
+                 lambda T, g2=g2: T["XT%d" % h][:, :, 16 * g2:16 * g2 + 16], g2 == 0, g2 == 1) for g2 in range(2)])
+        for q in range(C // 4):
+            for r4 in range(4):
+                mm(4 * 64, [("AX", h, 2 * q), ("AX", h, 2 * q + 1)] + LRall, [("bank", QD), ("D", h, q, r4)], [
+                    (lambda T, q=q: T[QD][:, 4 * q:4 * q + 4, :], lambda T, r=r: T.LR[:, r, :],
+                     lambda T, r=r, q=q: T["AX%d" % h][:, 4 * q:4 * q + 4, 16 * r:16 * r + 16], r == 0, r == 15) for r in range(4 * r4, 4 * r4 + 4)])
+
+    def mid(t, h):
+        HS = str(h)
+        RX, TX, MM, SM, LTB = "RX" + HS, "TX" + HS, "MM" + HS, "SM" + HS, "LT" + HS
+        x0, n0 = LH * t, 2 * LH * t
+        QC, QD, CL, RN = "QC" + HS, "QD" + HS, "CL" + HS, "RN" + HS
+        tl = lambda T: T["TL" + HS][:]
+        sm = lambda i: (lambda T: T[SM][:, i * LH:(i + 1) * LH])
+        lt = lambda i: (lambda T: T[LTB][:, 8 * i:8 * i + C])
+        ol = lambda T: T["OL" + HS][:]
+        ex = lambda T: T.EX[:]
+        bank = lambda b: ("bank", b)
+        q0 = h * 3 * LH
+        qs = lambda i: (lambda T: T[QC][:, i * LH:(i + 1) * LH])
+        st = lambda T: T.QU[:, q0:q0 + LH]
+        e0 = qs(2)
+        uu = lambda a_, b_: (lambda T: T.QU[:, q0 + LH * a_:q0 + LH * b_])
+        mk = lambda T: T[MM][:, 0:LH]
+        mo = lambda T: T[MM][:, LH:2 * LH]
+        tn = lambda T: T["TN" + HS][:, n0:n0 + LH]
+        dreg = [("D", h, q, r4) for q in range(C // 4) for r4 in range(4)]
+        ts(LH, [bank(QD)] + dreg + ["LM%d" % t], [("S1", h)], lambda T: T["S1" + HS][:], lambda T: T[QD][:, 0:C, :],
+           lambda T: T.LM[:, t:t + 1], None, A.max)
+        tt(LH // 2, [("S1", h), bank(QD), ("KN", h, 0), ("KN", h, 1)], [("S2", h)], lambda T: T["S2" + HS][:], lambda T: T["S1" + HS][:],
+           lambda T: T[QD][:, 16:16 + C, :], A.add)
+        v(LH, [("S2", h), "R2"], [("SC", h)], lambda E: E["g"].vector.tensor_tensor_scan(
+            E["T"]["SC" + HS][:], E["T"].R2[:], E["T"]["S2" + HS][:], 0.0, A.max, A.min))
+        sc = lambda T: T["SC" + HS][:, 15:LH:16]
+        ts(C, [("SC", h)], [("OI", h)], lambda T: T["OI" + HS][:], sc, 2047, None, A.bitwise_and)
+        tc(C, [("OI", h)], [("OL", h)], ol, lambda T: T["OI" + HS][:])
+        OLr = [("OL", h)]
+        tt(LH, OLr + KTall + [("MK", h)], [("HT", h)], lambda T: T["HT" + HS][:], lambda T: T.KT[:, 0:W].indirect(ol(T)), mk, A.is_equal, True)
+        ht = lambda T: T["HT" + HS][:]
+        mm(LH, [("HT", h), "PW"], [bank(QC), ("S", h)], [(qs(0), lambda T: T.PW[:], ht, True, True)])
+        tt(LH, [("HT", h), ("MO", h)], [("sm", h, 0)], sm(0), ht, mo, A.mult)
+        ts(LH, [bank(QC), ("S", h), cpy(THR)], [("sm", h, 1)], sm(1), qs(0), co(THR), None, A.is_lt)
+        tt(LH, [("sm", h, 0), ("sm", h, 1)], [("sm", h, 2)], sm(2), sm(1), sm(0), A.mult)
+        mm(5 * LH, [("sm", h, 2), "BF", "IB", "OD"], [bank(QC), ("e", h)], [
+            (e0, lambda T: T.IB[:], lambda T: T.OD[:], True, False), (e0, lambda T: T.BF[:], sm(2), False, True)])
+        mm(LH, [("HT", h), "PSa", "PSb"], [bank(QC), ("Sp", h)], [(qs(1), lambda T: T.PS_[:], ht, True, True)])
+        v(LH, [bank(QC), ("e", h), "R2"], [("sm", h, 3)], lambda E: E["g"].vector.tensor_tensor_scan(
+            sm(3)(E["T"]), E["T"].R2[:], e0(E["T"]), 0.0, A.max, A.min))
+        ev = lambda T: T[SM][:, 3 * LH + 15:4 * LH:16]
+        tc(C, [("sm", h, 3)], [("EL", h)], lambda T: T["EL" + HS][:], ev)
+        if t < STEPS - 1:
+            tt(LH, OLr + ["F", ("RXq", h, t)], [("sm", h, 8)], sm(8), lambda T: T.F[:, 0:W].indirect(ol(T)), lambda T: T[RX][:, x0:x0 + LH], A.subtract, True)
+            act(LH, [("sm", h, 8)], [("TXq", h, t)], lambda T: T[TX][:, x0:x0 + LH], sm(8), AF.Abs)
+            op("g", 1.0, [("TXq", h, t)], [("sent", "x", h, t)], lambda E: E["send"]("x", t, h), "send")
+            op("net", TRANSIT, [("sent", "x", h, t)], [("RXq", h, t + 1)], None, ("ax", t + 1, h))
+        act(LH * 1.5, OLr + ["IDT"], [("TL", h)], tl, lambda T: T.IDT[:, 0:W].indirect(ol(T)))
+        if t < STEPS - 1:
+            tc(LH, [("TL", h)], [("TNl", h, t)], lambda T: T["TN" + HS][:, n0 + LH:n0 + 2 * LH], tl)
+        ts(LH, [bank(QC), ("Sp", h)], [("sm", h, 4)], sm(4), qs(1), 0.0, None, A.is_le)
+        ts(LH, [bank(QC), ("Sp", h)], [("sm", h, 5)], sm(5), qs(1), 0.0, None, A.is_gt)
+        tt(LH, OLr + Kall + [("sm", h, 4)], [("sm", h, 6)], sm(6), lambda T: T.K[:, D0:KW].indirect(ol(T)), sm(4), A.mult, True)
+        tt(LH, [("EL", h), ("sm", h, 5)] + Kall, [("sm", h, 7)], sm(7), lambda T: T.K[:, 0:KW].indirect(T["EL" + HS][:]), sm(5), A.mult, True)
+        tt(LH, [("sm", h, 6), ("sm", h, 7)], [("TN", h, t)], tn, sm(7), sm(6), A.add)
+        op("g", 1.0, [("TN", h, t)] + ([("TNl", h, t)] if t < STEPS - 1 else []), [("sent", "n", h, t)], lambda E: E["send"]("n", t, h), "send")
+        op("net", TRANSIT, [("sent", "n", h, t)], [("RN", h, t + 1), ("RNl", h, t + 1)], None, ("an", t + 1, h))
+        if t < STEPS - 1:
+            a(LH + 150, [bank(QC), ("S", h)], [("CN", t, h), ("junk", h)], lambda E: E["g"].scalar.activation(
+                E["T"]["SB" + HS][:], qs(0)(E["T"]), AF.Sign, accum_out=E["T"].CN[:, t * H + h:t * H + h + 1]))
+        ts(C, [("SC", h), "LI%d" % t], [("lt", h, 0)], lt(0), sc, lambda T: T.LM[:, 8 + t:9 + t], None, A.is_ge)
+        tt(LH, [("lt", h, 0), "EX", "DG"], [("ND", h)], lambda T: T["ND" + HS][:], lambda T: lt(0)(T).indirect(ex(T)), lambda T: T.DG[:], A.mult, True)
+        mm(2 * LH, [("ND", h), ("PI", t)], [bank("QU"), ("U", h)], [
+            (uu(1, 2), lambda T: T.PI[:, t, :], lambda T: T["ND" + HS][:], True, True),
+            (uu(2, 3), lambda T: T.PI[:, t, :], lambda T: T["ND" + HS][:], True, True)])
+        act(LH * 1.5, OLr + KTall, [("CLc", h)], lambda T: T[CL][:, 0:LH], lambda T: T.KT[:, 0:W].indirect(ol(T)))
+        if t:
+            tc(LH, [("RNl", h, t)], [("CLl", h)], lambda T: T[CL][:, LH:2 * LH], lambda T: T[RN][:, n0 + LH:n0 + 2 * LH])
+        dd = lambda T: T["DD" + HS][:]
+        mall = lambda T: T[MM][:]
+        tt(2 * LH, [("CLc", h), ("CLl", h), ("MK", h), ("MO", h)], [("DD", h)], dd, lambda T: T[CL][:], mall, A.subtract)
+        tt(LH, [("DD", h), bank("QU"), ("U", h)], [("DD", h)], dd, dd, uu(1, 3), A.mult)
+        tt(2 * LH, [("DD", h)], [("MK", h), ("MO", h)], mall, mall, dd, A.add)
+        ts(C, [("OI", h)], [("lt", h, 1)], lt(1), lambda T: T["OI" + HS][:], float(D0), None, A.add)
+        tt(LH, [("lt", h, 1), "EX", ("TL", h)], [("sb", h, 0)], sm(9), lambda T: lt(1)(T).indirect(ex(T)), tl, A.not_equal, True)
+        mm(2 * LH, [("HT", h), "PW", "IB", "NT"], [bank("QU"), ("St", h)], [
+            (st, lambda T: T.IB[:], lambda T: T.NT[:], True, False), (st, lambda T: T.PW[:], ht, False, True)])
+        ts(LH, [bank("QU"), ("St", h)], [("sm", h, 10)], sm(10), st, 0.5, None, A.is_lt)
+        tt(LH, [("sm", h, 10), ("sb", h, 0)], [("sm", h, 10)], sm(10), sm(10), sm(9), A.max)
+        v(LH, [("sm", h, 10), "R2"], [("sm", h, 11)], lambda E: E["g"].vector.tensor_tensor_scan(
+            sm(11)(E["T"]), E["T"].R2[:], sm(10)(E["T"]), 0.0, A.max, A.min))
+        ts(C, [("sm", h, 3)], [("lt", h, 2)], lt(2), ev, float(D0), None, A.is_ge)
+        tt(C, [("lt", h, 2), ("lt", h, 1)], [("lt", h, 3)], lt(3), lt(2), lt(1), A.mult)
+        tt(C, [("lt", h, 3), ("sm", h, 11)], [("lt", h, 4)], lt(4), lt(3), lambda T: T[SM][:, 11 * LH + 15:12 * LH:16], A.mult)
+        ts(C, [("lt", h, 4), "PT"], [("SL", h)], lambda T: T["SL" + HS][:, 0:2 * C:2], lt(4), pm, None, A.max)
+
+    def scatters(t):
+        for h in reversed(range(H)):
+            for c in reversed(range(C)):
+                src = lambda T, h=h, c=c: T["TN%d" % h][:, 2 * LH * t + 16 * c:2 * LH * t + 16 * c + 16]
+                v(64, [("SL", h), ("TN", h, t)], Kall, lambda E, h=h, c=c, src=src: E["g"].vector.tensor_copy(
+                    E["T"].K[:, 0:KW].indirect(E["T"]["SL%d" % h][:, 2 * c:2 * c + 1]), src(E["T"])))
+
+    def count(t):
+        mm(256 * H, [("CN", t, h) for h in range(H)] + ["ON"], [("bank", "QU"), "cnt"], [
+            (lambda T: T.QU[:, 511:512], lambda T: T.ON[:], lambda T, h=h: T.CN[:, t * H + h:t * H + h + 1], h == 0, h == H - 1) for h in range(H)])
+        tc(1, [("bank", "QU"), "cnt"], [("CC", t)], lambda T: T.CC[:, t:t + 1], lambda T: T.QU[:, 511:512])
+        ts(1, [("CC", t)], [("CA", t)], lambda T: T.CA[:, t:t + 1], lambda T: T.CC[:, t:t + 1], 15, None, A.bitwise_and)
+        ts(1, [("CA", t)], ["LM%d" % (t + 1)], lambda T: T.LM[:, t + 1:t + 2], lambda T: T.CA[:, t:t + 1], 57.0, 32768.0, A.add, A.mult)
+        ts(1, [("CA", t)], ["LI%d" % (t + 1)], lambda T: T.LM[:, t + 9:t + 10], lambda T: T.CA[:, t:t + 1], 58.0, 32768.0, A.add, A.mult)
+
+    setup_rest()
+    for h in range(H):
+        front(0, h)
+        if h == 0:
+            for b in range(4):
+                keytable(b)
+            setup_late()
+    for t in range(STEPS):
+        for h in range(H):
+            if t:
+                front(t, h)
+            mid(t, h)
+        scatters(t)
+        if t < STEPS - 1:
+            count(t)
+    for h in range(H):
+        tc(LH, [("RN", h, STEPS)], [("YN", h)], lambda T, h=h: T.YN[:, h * LH:(h + 1) * LH], lambda T, h=h: T["RN%d" % h][:, 2 * STEPS * LH:(2 * STEPS + 1) * LH])
+    dma("dy", "oyn", [("YN", h) for h in range(H)], ["oyn"], lambda T: T.yn[:], lambda T: T.YN[:], 2.5)
+    for h in range(H):
+        ts(LH, [("MO", h)], [("ym", h)], lambda T, h=h: T.YM[:, h * LH:(h + 1) * LH], lambda T, h=h: T["MM%d" % h][:, LH:2 * LH], 64.0, -64.0 * D0, A.mult, A.add)
+        tt(LH, [("ym", h), ("MK", h)], [("ym", h)], lambda T, h=h: T.YM[:, h * LH:(h + 1) * LH], lambda T, h=h: T.YM[:, h * LH:(h + 1) * LH],
+           lambda T, h=h: T["MM%d" % h][:, 0:LH], A.add)
+    dma("dy", "oym", [("ym", h) for h in range(H)], ["oym"], lambda T: T.ymu[:], lambda T: T.YM[:], 2.5)
+    kb = lambda b: (lambda T: T.K[:, D0 + 256 * b:D0 + 256 * b + 256])
+    mm(4096, Kall + [("YI", b) for b in range(4)], [("bank", "X0")], [
+        (lambda T: T.X0[:, 0, :], lambda T, b=b: T.YI[:, b, :], kb(b), b == 0, b == 3) for b in range(4)])
+    for b in range(4, 8):
+        act(256, Kall, [("YS", b)], lambda T, b=b: T.YS[:, b - 4, :], kb(b), AF.Copy, float(b + 1))
+    yd = lambda T: T.YD[:]
+    tt(256, [("YS", 4), ("YS", 5)], ["YD"], yd, lambda T: T.YS[:, 0, :], lambda T: T.YS[:, 1, :], A.add)
+    tt(256, ["YD", ("YS", 6)], ["YD"], yd, yd, lambda T: T.YS[:, 2, :], A.add)
+    tt(256, ["YD", ("YS", 7)], ["YD"], yd, yd, lambda T: T.YS[:, 3, :], A.add)
+    tt(256, ["YD", ("bank", "X0")], ["YD"], yd, yd, lambda T: T.X0[:, 0, :], A.add)
+    dma("dy", "oyd", ["YD"], ["oyd"], lambda T: T.yd[:], yd, 2.5)
+    return nodes
+
+
+def plan():
+    nodes = build()
+    n = len(nodes)
+    deps = [dict() for _ in range(n)]
+    lastw, readers, banks = {}, {}, {}
+    for i, (q, us, R, Wr, fn, tag) in enumerate(nodes):
+        def need(j, hard):
+            if j != i:
+                deps[i][j] = deps[i].get(j, False) or hard
+        bk = set(k for k in R + Wr if isinstance(k, tuple) and k[0] == "bank")
+        for k in bk:
+            acc = banks.setdefault(k, [])
+            for j in acc:
+                if nodes[j][0] != q:
+                    need(j, True)
+            acc.append(i)
+        for k in R:
+            if k in bk:
+                if k in lastw:
+                    need(lastw[k], True)
+                continue
+            if k in lastw:
+                need(lastw[k], True)
+            readers.setdefault(k, []).append(i)
+        for k in Wr:
+            if k in bk:
+                if k in lastw and nodes[lastw[k]][0] == q:
+                    need(lastw[k], q != "t")
+                lastw[k] = i
+                continue
+            if k in lastw:
+                need(lastw[k], True)
+            for j in readers.get(k, []):
+                need(j, nodes[j][0] != q)
+            readers[k] = []
+            lastw[k] = i
+    succ = [[] for _ in range(n)]
+    for i in range(n):
+        for j in deps[i]:
+            succ[j].append(i)
+    prio = [0.0] * n
+    for i in reversed(range(n)):
+        prio[i] = nodes[i][1] + max([prio[j] + 0.08 for j in succ[i]] or [0.0])
+    left = [len(d) for d in deps]
+    fin, avail, order = [0.0] * n, {}, {}
+    ready = [i for i in range(n) if left[i] == 0]
+    seq = []
+
+    def est(i):
+        q = nodes[i][0]
+        e = avail.get(q, 0.0)
+        for j in deps[i]:
+            e = max(e, fin[j] + (0.1 if deps[i][j] else 0.0))
+        return e
+    while ready:
+        es = [(est(i), i) for i in ready]
+        lo = min(es)[0]
+        qb = nodes[min(es)[1]][0]
+        i = max((prio[i], -i) for e, i in es if nodes[i][0] == qb and e <= lo + 0.03)[1] * -1
+        e = est(i)
+        q = nodes[i][0]
+        ready.remove(i)
+        seq.append(i)
+        order.setdefault(q, []).append(i)
+        fin[i] = e + nodes[i][1]
+        avail[q] = e if q == "net" else (e + 0.1 if q in ("dy", "ds") else fin[i])
+        for j in succ[i]:
+            left[j] -= 1
+            if left[j] == 0:
+                ready.append(j)
+    real = {"v": "v", "a": "a", "ds": "a", "t": "t", "g": "g", "dy": "y"}
+    pos, cnt = {}, {}
+    for i in seq:
+        q, tag = nodes[i][0], nodes[i][5]
+        if q in CTR and tag != "send":
+            cnt[q] = cnt.get(q, 0) + 1
+            pos[i] = cnt[q]
+    known = {}
+    clock = {}
+    out = []
+    for i in seq:
+        q, tag = nodes[i][0], nodes[i][5]
+        if q == "net":
+            continue
+        rq = real[q]
+        kn = known.setdefault(rq, {})
+        waits = {}
+
+        for j in sorted(deps[i], key=lambda j: -pos.get(j, 0)):
+            if not deps[i][j]:
+                continue
+            qj, tj = nodes[j][0], nodes[j][5]
+            if qj == "net":
+                key, val = tj, 1
+            elif qj in ("dy", "ds"):
+                key, val = tj, 16
+            elif tj == "send":
+                continue
+            else:
+                key, val = qj, pos[j]
+            if kn.get(key, 0) < val and waits.get(key, (0, None))[0] < val:
+                waits[key] = (val, j)
+        for key in list(waits):
+            val, j = waits[key]
+            for k2 in list(waits):
+                if k2 != key and k2 in waits and key in waits and clock.get(waits[k2][1], {}).get(key, 0) >= val:
+                    del waits[key]
+                    break
+        for key, (val, j) in waits.items():
+            kn[key] = max(kn.get(key, 0), val)
+            for k2, v2 in clock.get(j, {}).items():
+                kn[k2] = max(kn.get(k2, 0), v2)
+        c = dict(kn)
+        if i in pos:
+            c[q] = max(c.get(q, 0), pos[i])
+        clock[i] = c
+        out.append((rq, q, nodes[i][4], tag, [(k, w[0]) for k, w in waits.items()]))
+    return out, cnt, (max(fin), seq, fin)
+
+
+CACHE = {}
+
+
+def route(core, dst, cores, topo):
+    if topo.may_write(core, dst):
+        return None
+    c = [x for x in topo.cores_of(core) if x not in cores and topo.may_write(x, dst)]
+    same = [x for x in c if topo.die(x) == topo.die(core)]
+    c = same or c
+    return {"x": c[0], "n": c[-1]}
+
+
+def bits(m):
+    return bin(m).count("1")
+
+
+def rank_program(g, core, T, topo):
+    cores = list(T.cores)
+    rank = T.rank_of(core)
+
+    def remote(p, out, in_, sem, dst):
+        rid, pid = topo.addr(dst, core)
+        g.remote_dma(out, in_, T.sem[sem], T.sem.ls, pid, rid, topo.mask(core, dst))
+        return bits(topo.mask(core, dst))
+
+    WX, WN = LH, 2 * LH
+
+    def piece(p, buf, k, t):
+        w = WX if p == "x" else WN
+        return T[buf][:, k * w:k * w + (LH if t == STEPS - 1 else w)]
+
+    if rank is None:
+        total = 0
+        jobs = []
+        for i, src in enumerate(cores):
+            dst = cores[(i + 1) % N]
+            ro = route(src, dst, cores, topo)
+            for p in ("x", "n"):
+                if ro and ro[p] == core:
+                    jobs.append((p, src, dst))
+        for t in range(STEPS):
+            for h in range(H):
+                for p, src, dst in jobs:
+                    if p == "x" and t == STEPS - 1:
+                        continue
+                    k = t * H + h
+                    buf = piece(p, "RY" + p.upper(), k, t)
+                    out = piece(p, "R%s%d" % (p.upper(), h), t + 1, t)
+                    sem = "a%s%d_%d" % (p, t + 1, h)
+                    g.wait_ge(T.sem[sem], bits(topo.mask(src, core)))
+                    total += remote(p, out, buf, sem, dst)
+        if total:
+            g.wait_ge(T.sem.ls, total)
+        return
+
+    if "p" not in CACHE:
+        CACHE["p"] = plan()
+    prog, cnt, _ = CACHE["p"]
+    nxt, prv = cores[(rank + 1) % N], cores[(rank - 1) % N]
+    ro_out, ro_in = route(core, nxt, cores, topo), route(prv, core, cores, topo)
+    tot = [0]
+
+    def send(p, t, h):
+        src = piece(p, "T%s%d" % (p.upper(), h), t, t)
+        sem = "a%s%d_%d" % (p, t + 1, h)
+        if ro_out is None:
+            tot[0] += remote(p, piece(p, "R%s%d" % (p.upper(), h), t + 1, t), src, sem, nxt)
+        else:
+            tot[0] += remote(p, piece(p, "RY" + p.upper(), t * H + h, t), src, sem, ro_out[p])
+
+    E = {"g": g, "T": T, "send": send}
+    eng = {"v": g.vector, "a": g.scalar, "t": g.tensor, "g": g, "y": g.sync}
+    for rq, q, fn, tag, waits in prog:
+        for key, val in waits:
+            if isinstance(key, tuple):
+                p, t, h = key
+                frm = prv if ro_in is None else ro_in[p[1]]
+                eng[rq].wait_ge(T.sem["%s%d_%d" % (p, t, h)], bits(topo.mask(frm, core)))
+            else:
+                eng[rq].wait_ge(T.sem[CTR[key] if key in CTR else key], val)
+        i = fn(E)
+        if tag == "send":
+            continue
+        i.then_inc(T.sem[CTR[q]] if q in CTR else T.sem[tag], 1 if q in CTR else 16)
+    for q in CTR:
+        g.wait_ge(T.sem[CTR[q]], cnt[q])
+    for n in DMAS:
+        g.wait_ge(T.sem["d_" + n], 16)
+    g.wait_ge(T.sem.ls, tot[0])

@@ -7,60 +7,63 @@ H = 2
 LH = L // H
 C = LH // 16
 NCH = LH // 32
-D0 = 128
+D0 = 16
+U0 = 4096
 KW = D0 + W
 BIG = 16777216.0
 RND = 12582912.0
-S_GATHER = {1: (0,), 2: (0,)}[H]
-TRANSIT = 5.0
+SC = 65536.0
+S_GATHER = ((0, 0), (0, 1))
+ON, OFF, LATX, LATS, BON, WIN = 5.0, 5.0, 0.1, 0.1, 0.0, 0.03
+ISSUE = 1.0
 
 SCRATCH = {
-    "F": ("sbuf", [128, W], "bfloat16"), "KI": ("sbuf", [128, W], "int32"), "K": ("sbuf", [128, KW], "float32"),
-    "KT": ("sbuf", [128, W], "bfloat16"), "IDT": ("sbuf", [128, W], "float32"), "HI": ("sbuf", [128, W], "bfloat16"),
-    "CI": ("sbuf", [128, L], "int32"), "LI": ("sbuf", [128, L], "int32"), "LF": ("sbuf", [128, L], "float32"),
-    "MKB": ("sbuf", [128, L], "bfloat16"), "MOI": ("sbuf", [128, L], "int32"),
-    "WI": ("sbuf", [128, 1], "int32"), "CST": ("sbuf", [128, 512], "bfloat16"),
-    "IM": ("sbuf", [128, 128], "float32"), "RI": ("sbuf", [128, 128], "float32"), "GI": ("sbuf", [128, 128], "float32"),
-    "PC": ("sbuf", [128, 8], "int32"), "PA": ("sbuf", [128, 8], "int32"), "PB": ("sbuf", [128, 8], "int32"),
-    "PT": ("sbuf", [128, 8], "float32"), "CO": ("sbuf", [128, 32], "float32"), "P2": ("sbuf", [128, 48], "float32"),
-    "IF": ("sbuf", [128, 128], "float32"), "IB": ("sbuf", [128, 128], "bfloat16"), "NI": ("sbuf", [128, 128], "bfloat16"),
-    "N64": ("sbuf", [128, 128], "bfloat16"), "BF": ("sbuf", [128, 128], "float32"), "RB": ("sbuf", [128, 128], "bfloat16"),
-    "RF": ("sbuf", [128, 128], "float32"), "WA": ("sbuf", [128, 128], "bfloat16"), "WC": ("sbuf", [128, 128], "bfloat16"),
-    "B8": ("sbuf", [128, 128], "float32"),
-    "LR": ("sbuf", [128, 16, 128], "bfloat16"), "PI": ("sbuf", [128, 8, 128], "bfloat16"),
-    "PW": ("sbuf", [128, 8, 16], "bfloat16"), "PS_": ("sbuf", [128, 8, 16], "bfloat16"), "B3": ("sbuf", [128, 8, 16], "float32"),
+    "F": ("sbuf", [128, KW], "bfloat16"), "KI": ("sbuf", [128, W], "int32"), "K": ("sbuf", [128, KW], "float32"),
+    "KT": ("sbuf", [128, KW], "bfloat16"), "IDT": ("sbuf", [128, KW], "float32"), "HI": ("sbuf", [128, W], "bfloat16"),
+    "WQ": ("sbuf", [128, 4, 512], "float32"), "CI": ("sbuf", [128, L], "int32"), "LI": ("sbuf", [128, L], "int32"),
+    "LF": ("sbuf", [128, L], "float32"), "MKB": ("sbuf", [128, L], "bfloat16"), "MOI": ("sbuf", [128, L], "int32"),
+    "WI": ("sbuf", [128, 1], "int32"), "IM": ("sbuf", [128, 128], "float32"), "RI": ("sbuf", [128, 128], "float32"),
+    "GI": ("sbuf", [128, 128], "float32"), "PC": ("sbuf", [128, 8], "int32"), "PA": ("sbuf", [128, 8], "int32"),
+    "PB": ("sbuf", [128, 8], "int32"), "PT": ("sbuf", [128, 8], "float32"), "CO": ("sbuf", [128, 32], "float32"),
+    "P2": ("sbuf", [128, 48], "float32"), "IF": ("sbuf", [128, 128], "float32"), "IB": ("sbuf", [128, 128], "bfloat16"),
+    "NI": ("sbuf", [128, 128], "bfloat16"), "N64": ("sbuf", [128, 128], "bfloat16"), "BF": ("sbuf", [128, 128], "float32"),
+    "RB": ("sbuf", [128, 128], "bfloat16"), "RF": ("sbuf", [128, 128], "float32"), "WC": ("sbuf", [128, 128], "bfloat16"),
+    "B8": ("sbuf", [128, 128], "float32"), "T1": ("sbuf", [128, 128], "float32"), "T2": ("sbuf", [128, 128], "float32"),
+    "T3": ("sbuf", [128, 128], "float32"), "LR": ("sbuf", [128, 16, 128], "bfloat16"), "PI": ("sbuf", [128, 8, 128], "bfloat16"),
+    "PW": ("sbuf", [128, 128], "bfloat16"), "PS_": ("sbuf", [128, 128], "bfloat16"), "PV": ("sbuf", [128, 128], "bfloat16"),
     "OD": ("sbuf", [128, LH], "bfloat16"), "NT": ("sbuf", [128, LH], "bfloat16"), "DG": ("sbuf", [128, LH], "float32"),
-    "R2": ("sbuf", [128, LH], "float32"), "SWM": ("sbuf", [128, 4, 128], "float32"),
-    "ON": ("sbuf", [128, 128], "float32"), "EXI": ("sbuf", [128, C], "int32"), "EX": ("sbuf", [128, C], "uint16"),
-    "ER": ("sbuf", [128, 16 * LH], "bfloat16"), "YI": ("sbuf", [128, 8, 128], "float32"),
+    "R2": ("sbuf", [128, LH], "float32"), "ON": ("sbuf", [128, 128], "float32"), "EXI": ("sbuf", [128, C], "int32"),
+    "EX": ("sbuf", [128, C], "uint16"), "ER": ("sbuf", [128, 16 * LH], "bfloat16"), "YI": ("sbuf", [128, 4, 128], "float32"),
     "CN": ("sbuf", [128, 32], "float32"), "CC": ("sbuf", [128, 16], "int32"), "CA": ("sbuf", [128, 16], "int32"),
-    "LM": ("sbuf", [128, 16], "float32"),
-    "YN": ("sbuf", [128, L], "float32"), "YM": ("sbuf", [128, L], "float32"), "YD": ("sbuf", [128, 256], "float32"),
-    "YS": ("sbuf", [128, 4, 256], "float32"),
+    "LM": ("sbuf", [128, 16], "float32"), "YN": ("sbuf", [128, L], "float32"), "YM": ("sbuf", [128, L], "float32"),
+    "YD": ("sbuf", [128, 256], "float32"), "YS": ("sbuf", [128, 4, 256], "float32"),
     "X0": ("psum", [128, 2, 256], "float32"), "X1": ("psum", [128, 2, 256], "float32"),
     "X2": ("psum", [128, 2, 256], "float32"), "QU": ("psum", [128, 512], "float32"),
-    "RYX": ("sbuf", [128, 7 * L], "bfloat16"), "RYN": ("sbuf", [128, 8 * 2 * L], "uint16"),
+    "RYX": ("sbuf", [128, 7 * L], "bfloat16"), "RYN": ("sbuf", [128, 16 * L], "uint16"),
 }
 for _h in range(H):
     SCRATCH["QD%d" % _h] = ("psum", [128, 32, 16], "float32")
     SCRATCH["QC%d" % _h] = ("psum", [128, 512], "float32")
-    for _n, _s, _d in (("RN", [128, 18 * LH], "uint16"), ("RX", [128, 8 * LH], "bfloat16"), ("TN", [128, 16 * LH], "uint16"),
-                       ("TX", [128, 8 * LH], "bfloat16"), ("TL", [128, LH], "float32"), ("CL", [128, 2 * LH], "float32"),
-                       ("MM", [128, 2 * LH], "float32"), ("QT", [128, 128], "bfloat16"),
-                       ("NF", [128, LH], "float32"), ("XT", [128, NCH, 32], "float32"), ("Z", [128, 16 * LH], "bfloat16"),
+    for _n, _s, _d in (("RN", [128, 27 * LH], "uint16"), ("RX", [128, 8 * LH], "bfloat16"), ("TN", [128, 24 * LH], "uint16"),
+                       ("TX", [128, 8 * LH], "bfloat16"), ("TL", [128, LH], "float32"),
+                       ("CL", [128, 2 * LH], "float32"), ("MM", [128, 2 * LH], "float32"), ("QT", [128, 128], "bfloat16"),
+                       ("NF", [128, C, 32], "float32"), ("XT", [128, C, 32], "float32"), ("Z", [128, 16 * LH], "bfloat16"),
                        ("AX", [128, C, 256], "bfloat16"), ("S1", [128, C, 16], "float32"), ("S2", [128, LH], "float32"),
-                       ("SC", [128, LH], "int32"), ("OI", [128, C], "int32"), ("OL", [128, C], "uint16"), ("HT", [128, LH], "bfloat16"),
-                       ("SM", [128, 12 * LH], "float32"), ("SB", [128, LH], "bfloat16"), ("LT", [128, 40], "float32"),
-                       ("EL", [128, C], "uint16"), ("SL", [128, 2 * C], "uint16"), ("ND", [128, LH], "bfloat16"),
-                       ("DD", [128, 2 * LH], "float32")):
+                       ("SC", [128, LH], "int32"), ("OI", [128, C], "int32"), ("OL", [128, C], "uint16"),
+                       ("HT", [128, LH], "bfloat16"), ("SM", [128, 12 * LH], "float32"), ("SB", [128, LH], "bfloat16"),
+                       ("LT", [128, 40], "float32"), ("EL", [128, C], "uint16"), ("SL", [128, 2 * C], "uint16"),
+                       ("ND", [128, LH], "bfloat16"), ("DD", [128, 2 * LH], "float32"), ("FO", [128, LH], "bfloat16")):
         SCRATCH[_n + str(_h)] = ("sbuf", _s, _d)
 
 DMAS = ["cand", "feat"] + ["want%d" % _h for _h in range(H)] + ["wts", "last", "mkey", "mobj", "kids", "oyn", "oym", "oyd"]
 SEMAPHORES = ["v", "a", "t", "gq", "ls"] + ["d_" + n for n in DMAS] + \
-    ["%s%d_%d" % (p, t, h) for p in ("ax", "an") for t in range(1, STEPS + (p == "an")) for h in range(H)]
+    ["a%s%d_%d" % (p, t, h) for p in ("x", "n") for t in range(1, STEPS + (p == "n")) for h in range(H)]
 
 CTR = {"v": "v", "a": "a", "t": "t", "g": "gq"}
-PM, PWC, THR, KCC, SG1, SG2, PF, PG, B4, TG = 0, 1, 2, 3, 4, 5, 6, 7, 8, 9
+PWC, DSG, KCC, SG1, SG2, PF, PG, B4, B5, QB = 1, 2, 3, 4, 5, 6, 7, 8, 9, 10
+PATH = ("Z", "xq", "xd", "AX", "D", "KN", "XT", "NF", "S1", "S2", "SC", "OI", "OL", "HT", "S", "Sp", "sm", "e", "EL", "TN", "TXq",
+        "qt", "QT", "sent", "FO", "qd")
+SETUP = [0]
 
 
 def build():
@@ -75,44 +78,26 @@ def build():
     def a(n, R, Wr, fn):
         op("a", 0.06 + max(64, n) * 0.00104, R, Wr, fn)
 
-    def t_(cyc, R, Wr, fn):
-        op("t", 0.03 + cyc * 0.0007, R, Wr, fn)
-
     def gq(n, Wr, fn):
         op("g", 0.15 + n * 0.0017, [], Wr, fn)
 
     def dma(q, name, R, Wr, out, in_, us=3.0):
         op(q, us, R, Wr, lambda E: (E["g"].sync if q == "dy" else E["g"].scalar).dma_start(out(E["T"]), in_(E["T"])), "d_" + name)
 
-    dma("dy", "cand", [], ["CI"], lambda T: T.CI[:], lambda T: T.cand[:], 2.5)
-    dma("ds", "wts", [], ["WI"], lambda T: T.WI[:], lambda T: T.wts[:], 2.5)
-    dma("dy", "feat", [], ["F"], lambda T: T.F[:], lambda T: T.feat[:], 5.0)
-    for h in range(H):
-        dma("ds", "want%d" % h, [], [("RXq", h, 0)], lambda T, h=h: T["RX%d" % h][:, 0:LH], lambda T, h=h: T.want[:, h * LH:(h + 1) * LH], 3.0)
-    dma("dy", "last", [], ["LI"], lambda T: T.LI[0:8, :], lambda T: T.last[:], 5.5)
-    dma("ds", "mkey", [], ["MKB"], lambda T: T.MKB[:], lambda T: T.mkey[:], 5.5)
-    dma("dy", "mobj", [], ["MOI"], lambda T: T.MOI[:], lambda T: T.mobj[:], 6.0)
-    dma("ds", "kids", [], ["KI"], lambda T: T.KI[:], lambda T: T.kids[:], 8.0)
-
-    gq(8, ["PC"], lambda E: E["g"].iota(E["T"].PC[:], [[5, 8]], 0, 1))
-    gq(128, ["IM"], lambda E: E["g"].iota(E["T"].IM[:], [[1, 128]], 0, 0, allow_small_or_imprecise_dtypes=True))
-    gq(128, ["RI"], lambda E: E["g"].iota(E["T"].RI[:], [[0, 8], [1, 16]], 0, 0, allow_small_or_imprecise_dtypes=True))
-    gq(128, ["GI"], lambda E: E["g"].iota(E["T"].GI[:], [[1, 8], [0, 16]], 0, 0, allow_small_or_imprecise_dtypes=True))
-    gq(C, ["EXI"], lambda E: E["g"].iota(E["T"].EXI[:], [[1, C]], 0, 0))
-    gq(W, ["IDT"], lambda E: E["g"].iota(E["T"].IDT[:], [[1, W]], D0, 0, allow_small_or_imprecise_dtypes=True))
+    def val(E, x):
+        return x if isinstance(x, (int, float)) or x is None else x(E["T"])
 
     def ts(n, R, Wr, out, in0, s1, s2, o0, o1=None):
         if o1 is None:
-            v(n, R, Wr, lambda E: E["g"].vector.tensor_scalar(out(E["T"]), in0(E["T"]), s1(E["T"]) if callable_(s1) else s1, None, o0))
+            v(n, R, Wr, lambda E: E["g"].vector.tensor_scalar(out(E["T"]), in0(E["T"]), val(E, s1), None, o0))
         else:
-            v(n, R, Wr, lambda E: E["g"].vector.tensor_scalar(out(E["T"]), in0(E["T"]), s1(E["T"]) if callable_(s1) else s1,
-                                                              s2(E["T"]) if callable_(s2) else s2, o0, o1))
+            v(n, R, Wr, lambda E: E["g"].vector.tensor_scalar(out(E["T"]), in0(E["T"]), val(E, s1), val(E, s2), o0, o1))
 
-    def callable_(x):
-        return not isinstance(x, (int, float))
+    def tt(n, R, Wr, out, in0, in1, o):
+        v(n * 2, R, Wr, lambda E: E["g"].vector.tensor_tensor(out(E["T"]), in0(E["T"]), in1(E["T"]), o))
 
-    def tt(n, R, Wr, out, in0, in1, o, ind=False):
-        v(n * 2 if not ind else int(n * 2), R, Wr, lambda E: E["g"].vector.tensor_tensor(out(E["T"]), in0(E["T"]), in1(E["T"]), o))
+    def scan(n, R, Wr, out, d0, d1, init, o0, o1):
+        v(n, R, Wr, lambda E: E["g"].vector.tensor_tensor_scan(out(E["T"]), d0(E["T"]), d1(E["T"]), init, o0, o1))
 
     def tc(n, R, Wr, out, in_):
         v(n, R, Wr, lambda E: E["g"].vector.tensor_copy(out(E["T"]), in_(E["T"])))
@@ -129,7 +114,7 @@ def build():
             for out, l, r, st, sp in calls:
                 i = E["g"].tensor.matmul(out(E["T"]), l(E["T"]), r(E["T"]), st, sp)
             return i
-        t_(cyc, R, Wr, emit)
+        op("t", 0.03 + cyc * 0.0007, R, Wr, emit)
 
     def co(i):
         return lambda T: T.CO[:, i:i + 1]
@@ -137,253 +122,258 @@ def build():
     def cpy(i):
         return "co%d" % i
 
+    def whole(n):
+        return lambda T: T[n][:]
+
+    dma("dy", "cand", [], ["CI"], whole("CI"), lambda T: T.cand[:], 2.5)
+    dma("ds", "wts", [], ["WI"], whole("WI"), lambda T: T.wts[:], 2.5)
+    dma("dy", "feat", [], ["F"], lambda T: T.F[:, D0:KW], lambda T: T.feat[:], 5.0)
     for h in range(H):
-        tc(LH, ["CI"], [("RN", h, 0), ("RNl", h, 0)], lambda T, h=h: T["RN%d" % h][:, 0:LH], lambda T, h=h: T.CI[:, h * LH:(h + 1) * LH])
-    ts(8, ["PC"], ["PA"], lambda T: T.PA[:], lambda T: T.PC[:], 15, None, A.bitwise_and)
-    tc(8, ["PA"], ["PT"], lambda T: T.PT[:], lambda T: T.PA[:])
+        dma("ds", "want%d" % h, [], [("RXq", h, 0)], lambda T, h=h: T["RX%d" % h][:, 0:LH], lambda T, h=h: T.want[:, h * LH:(h + 1) * LH], 3.0)
+    dma("dy", "last", [], ["LI"], lambda T: T.LI[0:8, :], lambda T: T.last[:], 5.5)
+    dma("ds", "mkey", [], ["MKB"], whole("MKB"), lambda T: T.mkey[:], 5.5)
+    dma("dy", "mobj", [], ["MOI"], whole("MOI"), lambda T: T.mobj[:], 6.0)
+    dma("ds", "kids", [], ["KI"], whole("KI"), lambda T: T.kids[:], 8.0)
+
+    def iota(n, name, pattern, base, cm, flag=True):
+        if flag:
+            gq(n, [name], lambda E: E["g"].iota(E["T"][name][:], pattern, base, cm, allow_small_or_imprecise_dtypes=True))
+        else:
+            gq(n, [name], lambda E: E["g"].iota(E["T"][name][:], pattern, base, cm))
+    iota(8, "PC", [[5, 8]], 0, 1, False)
+    iota(128, "IM", [[1, 128]], 0, 0)
+    iota(128, "RI", [[0, 8], [1, 16]], 0, 0)
+    iota(128, "GI", [[1, 8], [0, 16]], 0, 0)
+    iota(C, "EXI", [[1, C]], 0, 0, False)
+    iota(KW, "IDT", [[1, KW]], 0, 0)
+    for h in range(H):
+        tc(LH, ["CI"], [("RN", h, 0)], lambda T, h=h: T["RN%d" % h][:, 0:LH], lambda T, h=h: T.CI[:, h * LH:(h + 1) * LH])
+    ts(8, ["PC"], ["PA"], whole("PA"), whole("PC"), 15, None, A.bitwise_and)
+    tc(8, ["PA"], ["PT"], whole("PT"), whole("PA"))
     tc(1, ["PC"], [cpy(PF)], co(PF), lambda T: T.PC[:, 0:1])
     ts(1, ["PC"], ["PB0"], lambda T: T.PB[:, 0:1], lambda T: T.PC[:, 0:1], 4, None, A.arith_shift_right)
     tc(1, ["PB0"], [cpy(PG)], co(PG), lambda T: T.PB[:, 0:1])
     ts(1, ["PB0"], ["PB1"], lambda T: T.PB[:, 1:2], lambda T: T.PB[:, 0:1], 1, None, A.bitwise_and)
     tc(1, ["PB1"], [cpy(B4)], co(B4), lambda T: T.PB[:, 1:2])
     pm = lambda T: T.PT[:, 0:1]
-    ts(128, ["IM", cpy(PF)], ["IF"], lambda T: T.IF[:], lambda T: T.IM[:], co(PF), None, A.is_equal)
-    ts(128, ["IM", cpy(PF)], ["NI"], lambda T: T.NI[:], lambda T: T.IM[:], co(PF), -1.0, A.is_equal, A.mult)
-    ts(128, ["IM", cpy(PF)], ["IB"], lambda T: T.IB[:], lambda T: T.IM[:], co(PF), None, A.is_equal)
-    ts(128, ["GI", cpy(PG)], ["BF"], lambda T: T.BF[:], lambda T: T.GI[:], co(PG), None, A.is_equal)
+    ts(128, ["IM", cpy(PF)], ["IF"], whole("IF"), whole("IM"), co(PF), None, A.is_equal)
+    ts(128, ["IM", cpy(PF)], ["NI"], whole("NI"), whole("IM"), co(PF), -1.0, A.is_equal, A.mult)
+    ts(128, ["IM", cpy(PF)], ["IB"], whole("IB"), whole("IM"), co(PF), None, A.is_equal)
+    ts(128, ["GI", cpy(PG)], ["BF"], whole("BF"), whole("GI"), co(PG), None, A.is_equal)
     for k in range(16):
-        tc(LH, ["IB"], [("ER", k)], lambda T, k=k: T.ER[:, k:16 * LH:16], lambda T: T.IB[:, 0:LH])
+        act(LH, ["IB"], [("ER", k)], lambda T, k=k: T.ER[:, k:16 * LH:16], lambda T: T.IB[:, 0:LH])
     ERall = [("ER", k) for k in range(16)]
-    ts(128, ["GI", cpy(PG)], ["RF"], lambda T: T.RF[:], lambda T: T.GI[:], co(PG), 100.0, A.not_equal, A.mult)
-    tt(128, ["RF", "RI"], ["RB"], lambda T: T.RB[:], lambda T: T.RF[:], lambda T: T.RI[:], A.add)
+    ts(128, ["GI", cpy(PG)], ["RF"], whole("RF"), whole("GI"), co(PG), 100.0, A.not_equal, A.mult)
+    tt(128, ["RF", "RI"], ["RB"], whole("RB"), whole("RF"), whole("RI"), A.add)
     for r in range(16):
-        ts(64, ["RB"], [("LR", r)], lambda T, r=r: T.LR[:, r, :], lambda T: T.RB[:], float(r), 32768.0, A.is_equal, A.mult)
+        ts(64, ["RB"], [("LR", r)], lambda T, r=r: T.LR[:, r, :], whole("RB"), float(r), SC, A.is_equal, A.mult)
     LRall = [("LR", r) for r in range(16)]
-    tc(1, ["WI"], [cpy(16)], co(16), lambda T: T.WI[:])
-    ts(128, ["BF", cpy(16)], ["WA"], lambda T: T.WA[:], lambda T: T.BF[:], co(16), 1.0 / 64, A.mult, A.mult)
-    ts(128, ["BF", cpy(16)], ["WC"], lambda T: T.WC[:], lambda T: T.BF[:], co(16), None, A.mult)
-    ts(128, ["IF"], ["N64"], lambda T: T.N64[:], lambda T: T.IF[:], -64.0, None, A.mult)
-    ms(256, ["CST"], lambda T: T.CST[:], -63.0 / 128)
+    tc(1, ["WI"], [cpy(16)], co(16), whole("WI"))
+    ts(128, ["BF", cpy(16)], ["WC"], whole("WC"), whole("BF"), co(16), None, A.mult)
+    ts(128, ["IF"], ["N64"], whole("N64"), whole("IF"), -64.0, None, A.mult)
+    ms(1, [cpy(QB)], co(QB), -63.0 / 128)
 
     def keytable(b):
-        sl = slice(512 * b, 512 * b + 512)
-        XB = "X%d" % ((b + 1) % 3)
-        mm(1024, ["WA", "F", "IB", "CST"], [("bank", XB)], [
-            (lambda T, j=j: T[XB][:, j, :], lambda T: T.IB[:], lambda T, j=j: T.CST[:, 256 * j:256 * j + 256], True, False) if s == 0 else
-            (lambda T, j=j: T[XB][:, j, :], lambda T: T.WA[:], lambda T, j=j: T.F[:, 512 * b + 256 * j:512 * b + 256 * j + 256], False, True)
-            for j in range(2) for s in range(2)])
+        X = "X%d" % ((b + 1) % 3)
+        xs = lambda j: (lambda T: T[X][:, j, :])
+        fs = lambda j: (lambda T: T.F[:, D0 + 512 * b + 256 * j:D0 + 512 * b + 256 * j + 256])
+        hs = lambda j: (lambda T: T.HI[:, 512 * b + 256 * j:512 * b + 256 * j + 256])
+        wq = lambda j: (lambda T: T.WQ[:, b, 256 * j:256 * j + 256])
+        mm(512, ["WC", "F"], [("bank", X)], [(xs(j), whole("WC"), fs(j), True, True) for j in range(2)])
         for j in range(2):
-            ts(256, [("bank", XB)], [("HI", b, j)], lambda T, j=j: T.HI[:, 512 * b + 256 * j:512 * b + 256 * j + 256],
-               lambda T, j=j: T[XB][:, j, :], RND, RND, A.add, A.subtract)
-        mm(1024, ["WC", "F", "N64", ("HI", b, 0), ("HI", b, 1)], [("bank", XB)], [
-            (lambda T, j=j: T[XB][:, j, :], lambda T: T.WC[:], lambda T, j=j: T.F[:, 512 * b + 256 * j:512 * b + 256 * j + 256], True, False) if s == 0 else
-            (lambda T, j=j: T[XB][:, j, :], lambda T: T.N64[:], lambda T, j=j: T.HI[:, 512 * b + 256 * j:512 * b + 256 * j + 256], False, True)
-            for j in range(2) for s in range(2)])
+            a(256, [("bank", X), cpy(QB)], [("WQ", b, j)], lambda E, j=j: E["g"].scalar.activation(
+                wq(j)(E["T"]), xs(j)(E["T"]), AF.Identity, bias=co(QB)(E["T"]), scale=1.0 / 64))
+            ts(256, [("WQ", b, j)], [("HI", b, j)], hs(j), wq(j), RND, RND, A.add, A.subtract)
+        mm(1024, ["WC", "F", "N64", ("HI", b, 0), ("HI", b, 1)], [("bank", X)], [
+            c for j in range(2) for c in ((xs(j), whole("WC"), fs(j), True, False), (xs(j), whole("N64"), hs(j), False, True))])
         for j in range(2):
-            act(256, [("bank", XB)], [("KT", b, j)], lambda T, j=j: T.KT[:, 512 * b + 256 * j:512 * b + 256 * j + 256], lambda T, j=j: T[XB][:, j, :])
-    KTall = [("KT", b, j) for b in range(4) for j in range(2)]
+            act(256, [("bank", X)], [("KT", b, j)], lambda T, j=j: T.KT[:, D0 + 512 * b + 256 * j:D0 + 512 * b + 256 * j + 256], xs(j))
+    KTall = ["KTd"] + [("KT", b, j) for b in range(4) for j in range(2)]
 
     def setup_rest():
         ms(1, ["P2a"], lambda T: T.P2[:, 0:16], 0.5)
         ms(1, ["P2b"], lambda T: T.P2[:, 16:32], 0.0)
-        v(16, ["P2a", "P2b"], ["P2c"], lambda E: E["g"].vector.tensor_tensor_scan(
-            E["T"].P2[:, 32:48], E["T"].P2[:, 0:16], E["T"].P2[:, 16:32], 65536.0, A.mult, A.add))
-        ts(64, ["RI", "PT"], ["DG"], lambda T: T.DG[:], lambda T: T.RI[:, 0:LH], pm, None, A.is_equal)
+        scan(16, ["P2a", "P2b"], ["P2c"], lambda T: T.P2[:, 32:48], lambda T: T.P2[:, 0:16], lambda T: T.P2[:, 16:32], 65536.0, A.mult, A.add)
+        ts(64, ["RI", "PT"], ["DG"], whole("DG"), lambda T: T.RI[:, 0:LH], pm, None, A.is_equal)
         tt(16, ["P2c", "DG"], ["P2a"], lambda T: T.P2[:, 0:16], lambda T: T.P2[:, 32:48], lambda T: T.DG[:, 0:16], A.mult)
         v(16, ["P2a"], [cpy(PWC)], lambda E: E["g"].vector.tensor_reduce(
             E["T"].CO[:, PWC:PWC + 1], E["T"].P2[:, 0:16], AxisListType.X, A.add))
-        ts(1, [cpy(PWC)], [cpy(THR)], co(THR), co(PWC), 2.0, None, A.mult)
-        ts(1, ["PT"], [cpy(KCC)], co(KCC), pm, 2048.0, None, A.mult)
+        ts(1, ["PT"], [cpy(KCC)], co(KCC), pm, 4096.0, float(D0), A.mult, A.add)
         ts(1, ["PT"], [cpy(17)], co(17), pm, 9.0, -2.0, A.is_ge, A.mult)
         ts(1, ["PT"], [cpy(18)], co(18), pm, 3.0, -2.0, A.is_ge, A.mult)
         ts(1, [cpy(17)], [cpy(19)], co(19), co(17), 1.0, None, A.add)
         tt(1, [cpy(18), cpy(17)], [cpy(20)], co(20), co(18), co(17), A.subtract)
         ts(1, [cpy(20)], [cpy(22)], co(22), co(20), 1.0, None, A.add)
-        v(1, [cpy(19), cpy(PWC)], [cpy(SG1)], lambda E: E["g"].vector.tensor_tensor(E["T"].CO[:, SG1:SG1 + 1], E["T"].CO[:, 19:20], E["T"].CO[:, PWC:PWC + 1], A.mult))
-        v(1, [cpy(22), cpy(PWC)], [cpy(SG2)], lambda E: E["g"].vector.tensor_tensor(E["T"].CO[:, SG2:SG2 + 1], E["T"].CO[:, 22:23], E["T"].CO[:, PWC:PWC + 1], A.mult))
-        for g8 in range(8):
-            tc(16, ["BF"], [("B3", g8)], lambda T, g8=g8: T.B3[:, g8, :], lambda T, g8=g8: T.BF[:, 16 * g8:16 * g8 + 16])
-        B3 = [("B3", g8) for g8 in range(8)]
-        ts(128, B3 + [cpy(PWC)], ["PW"], lambda T: T.PW[:], lambda T: T.B3[:], co(PWC), None, A.mult)
-        ts(64, B3 + [cpy(SG1)], ["PSa"], lambda T: T.PS_[:, :, 0:8], lambda T: T.B3[:, :, 0:8], co(SG1), None, A.mult)
-        ts(64, B3 + [cpy(SG2)], ["PSb"], lambda T: T.PS_[:, :, 8:16], lambda T: T.B3[:, :, 8:16], co(SG2), None, A.mult)
-        ts(64, ["RI", "PT"], ["OD"], lambda T: T.OD[:], lambda T: T.RI[:, 0:LH], pm, 8192.0, A.not_equal, A.mult)
-        ts(64, ["RI", "PT"], ["NT"], lambda T: T.NT[:], lambda T: T.RI[:, 0:LH], pm, -131072.0, A.is_ge, A.mult)
-        tc(C, ["EXI"], ["EX"], lambda T: T.EX[:], lambda T: T.EXI[:])
-        ts(64, ["RI"], ["R2"], lambda T: T.R2[:], lambda T: T.RI[:, 0:LH], 0.0, BIG, A.is_equal, A.mult)
-        for g2 in range(2):
-            for c2 in range(2):
-                i = 2 * g2 + c2
-                ts(1, [cpy(PF)], [cpy(23 + i)], co(23 + i), co(PF), float(16 * (g2 - c2) + 1), None, A.add)
-                ts(1, [cpy(B4)], [cpy(27 + i)], co(27 + i), co(B4), float(c2), None, A.is_equal)
-                tt(1, [cpy(23 + i), cpy(27 + i)], [cpy(TG + i)], co(TG + i), co(23 + i), co(27 + i), A.mult)
-                ts(1, [cpy(TG + i)], [("tg", i)], co(TG + i), co(TG + i), -1.0, None, A.add)
-                ts(128, [("tg", i), "IM"], [("SWM", i)], lambda T, i=i: T.SWM[:, i, :], lambda T: T.IM[:], co(TG + i), None, A.is_equal)
+        tt(1, [cpy(19), cpy(PWC)], [cpy(SG1)], co(SG1), co(19), co(PWC), A.mult)
+        tt(1, [cpy(22), cpy(PWC)], [cpy(SG2)], co(SG2), co(22), co(PWC), A.mult)
+        tt(1, [cpy(SG2), cpy(SG1)], [cpy(DSG)], co(DSG), co(SG2), co(SG1), A.subtract)
+        ts(128, ["RI"], ["T1"], whole("T1"), whole("RI"), 0.0, 2.0, A.is_gt, A.mult)
+        ts(128, ["RI"], ["T2"], whole("T2"), whole("RI"), 0.0, 2.0 ** -16, A.is_equal, A.mult)
+        scan(128, ["T1", "T2"], ["T3"], whole("T3"), whole("T1"), whole("T2"), 0.0, A.mult, A.add)
+        ts(128, ["BF", cpy(PWC)], ["T2"], whole("T2"), whole("BF"), co(PWC), None, A.mult)
+        tt(128, ["T2", "T3"], ["PW"], whole("PW"), whole("T2"), whole("T3"), A.mult)
+        ts(128, ["T2"], ["PV"], whole("PV"), whole("T2"), 2.0 ** -16, None, A.mult)
+        ts(128, ["RI"], ["T1"], whole("T1"), whole("RI"), 8.0, None, A.is_ge)
+        ts(128, ["T1", cpy(DSG), cpy(SG1)], ["T1"], whole("T1"), whole("T1"), co(DSG), co(SG1), A.mult, A.add)
+        tt(128, ["T1", "BF"], ["PSa"], whole("PS_"), whole("T1"), whole("BF"), A.mult)
+        ts(64, ["RI", "PT"], ["OD"], whole("OD"), lambda T: T.RI[:, 0:LH], pm, 8192.0, A.not_equal, A.mult)
+        ts(64, ["RI", "PT"], ["NT"], whole("NT"), lambda T: T.RI[:, 0:LH], pm, -131072.0, A.is_ge, A.mult)
+        tc(C, ["EXI"], ["EX"], whole("EX"), whole("EXI"))
+        ts(64, ["RI"], ["R2"], whole("R2"), lambda T: T.RI[:, 0:LH], 0.0, BIG, A.is_equal, A.mult)
+        ts(1, [cpy(B4)], [cpy(B5)], co(B5), co(B4), -1.0, 1.0, A.mult, A.add)
 
     def setup_late():
         for h in range(H):
             tc(LH, ["MKB"], [("MK", h)], lambda T, h=h: T["MM%d" % h][:, 0:LH], lambda T, h=h: T.MKB[:, h * LH:(h + 1) * LH])
-            ts(LH, ["MOI"], [("MO", h)], lambda T, h=h: T["MM%d" % h][:, LH:2 * LH], lambda T, h=h: T.MOI[:, h * LH:(h + 1) * LH], float(D0), None, A.add)
-        ms(128, ["Kd"], lambda T: T.K[:, 0:D0], 0.0)
+            ts(LH, ["MOI"], [("MO", h)], lambda T, h=h: T["MM%d" % h][:, LH:2 * LH], lambda T, h=h: T.MOI[:, h * LH:(h + 1) * LH], float(U0), None, A.add)
+        ms(16, ["Kd"], lambda T: T.K[:, 0:D0], 0.0)
         for b in range(4):
             tc(512, ["KI"], [("Kb", b)], lambda T, b=b: T.K[:, D0 + 512 * b:D0 + 512 * b + 512], lambda T, b=b: T.KI[:, 512 * b:512 * b + 512])
         for t in range(8):
-            ts(128, ["RB", "PT"], [("PI", t)], lambda T, t=t: T.PI[:, t, :], lambda T: T.RB[:], lambda T, t=t: T.PT[:, t:t + 1], None, A.is_equal)
-        ms(128, ["ON"], lambda T: T.ON[:], 1.0 / 16)
+            ts(128, ["RB", "PT"], [("PI", t)], lambda T, t=t: T.PI[:, t, :], whole("RB"), lambda T, t=t: T.PT[:, t:t + 1], None, A.is_equal)
+        ms(128, ["ON"], whole("ON"), 1.0 / 16)
         tc(128, ["LI"], ["LF"], lambda T: T.LF[0:8, :], lambda T: T.LI[0:8, :])
-        ts(128, ["GI", cpy(PF)], ["B8"], lambda T: T.B8[:], lambda T: T.GI[:], co(PF), None, A.is_equal)
+        ts(128, ["GI", cpy(PF)], ["B8"], whole("B8"), whole("GI"), co(PF), None, A.is_equal)
         mm(512, ["B8", "LF"], [("bank", "QU")], [(lambda T: T.QU[:, 0:128], lambda T: T.B8[0:8, :], lambda T: T.LF[0:8, :], True, True)])
         for h in range(H):
-            ts(LH, [("bank", "QU")], [("CLl", h)], lambda T, h=h: T["CL%d" % h][:, LH:2 * LH], lambda T, h=h: T.QU[:, h * LH:(h + 1) * LH], float(D0), None, A.add)
-        for b in range(8):
-            ts(128, ["IF"], [("YI", b)], lambda T, b=b: T.YI[:, b, :], lambda T: T.IF[:], float(b + 1), None, A.mult)
+            ts(LH, [("bank", "QU")], [("CLl", h)], lambda T, h=h: T["CL%d" % h][:, LH:2 * LH], lambda T, h=h: T.QU[:, h * LH:(h + 1) * LH], float(U0), None, A.add)
+        for b in range(4):
+            act(128, ["IF"], [("YI", b)], lambda T, b=b: T.YI[:, b, :], whole("IF"), AF.Copy, float(b + 1))
 
-    ms(1, ["LM0"], lambda T: T.LM[:, 0:1], 57.0 * 32768)
-    ms(1, ["LI0"], lambda T: T.LM[:, 8:9], 58.0 * 32768)
+    ms(1, ["LM0"], lambda T: T.LM[:, 0:1], 57.0 * SC)
+    ms(1, ["Fd"], lambda T: T.F[:, 0:D0], 0.0)
+    ms(1, ["KTd"], lambda T: T.KT[:, 0:D0], 0.0)
     Kall = ["Kd"] + [("Kb", b) for b in range(4)] + ["K"]
 
     def front(t, h):
-        RN, RX = "RN%d" % h, "RX%d" % h
-        QC, QD = "QC%d" % h, "QD%d" % h
+        RN, RX, QC, QD, Z, AX = ("%s%d" % (x, h) for x in ("RN", "RX", "QC", "QD", "Z", "AX"))
+        n0 = 2 * LH * t
         mm(128, [("RXq", h, t), "IB"], [("bank", QC), ("qt", h)], [
-            (lambda T: T[QC][0:LH, 384:512], lambda T: T[RX][:, LH * t:LH * t + LH], lambda T: T.IB[:], True, True)])
+            (lambda T: T[QC][0:LH, 384:512], lambda T: T[RX][:, LH * t:LH * t + LH], whole("IB"), True, True)])
         act(128, [("bank", QC), ("qt", h)], [("QT", h)], lambda T: T["QT%d" % h][0:LH, :], lambda T: T[QC][0:LH, 384:512])
-        ts(LH, [("RN", h, t), cpy(KCC)], [("NF", h)], lambda T: T["NF%d" % h][:], lambda T: T[RN][:, 2 * LH * t:2 * LH * t + LH], co(KCC), None, A.add)
+        for g2 in range(2):
+            ts(LH, [("RN", h, t), cpy(KCC), cpy(B5), cpy(B4)], [("NF", h, g2)], lambda T, g2=g2: T["NF%d" % h][:, :, 16 * g2:16 * g2 + 16],
+               lambda T: T[RN][:, n0:n0 + LH], co(KCC), co(B4 if g2 else B5), A.add, A.mult)
 
         def turn(E):
             i = None
-            for b in range(NCH):
-                i = E["g"].vector.transpose(E["T"]["XT%d" % h][:, b, :], E["T"]["NF%d" % h][:, 32 * b:32 * b + 32])
+            for c in range(C):
+                i = E["g"].vector.transpose(E["T"]["XT%d" % h][:, c, :], E["T"]["NF%d" % h][:, c, :])
             return i
-        v(64 * NCH, [("NF", h)], [("XT", h)], turn)
+        v(64 * C, [("NF", h, 0), ("NF", h, 1)], [("XT", h)], turn)
+        tt(LH, [("XT", h)], [("bank", QD), ("KN", h)], lambda T: T[QD][:, 16:16 + C, :], lambda T: T["XT%d" % h][:, :, 0:16],
+           lambda T: T["XT%d" % h][:, :, 16:32], A.add)
         for m in range(NCH):
             zs = slice(512 * m, 512 * m + 512)
-            XB = "X%d" % ((h * NCH + m) % 3)
+            X = "X%d" % ((h * NCH + m) % 3)
             for j in range(2):
-                cols = slice(2 * LH * t + 32 * m + 16 * j, 2 * LH * t + 32 * m + 16 * j + 16)
+                cols = slice(n0 + 32 * m + 16 * j, n0 + 32 * m + 16 * j + 16)
                 z2 = slice(512 * m + 256 * j, 512 * m + 256 * j + 256)
-                if m in S_GATHER:
-                    a(256 * 1.5 + 60, ["F", ("RN", h, t)], [("Z", h, m, j)], lambda E, zs=z2, cols=cols: E["g"].scalar.activation(
-                        E["T"]["Z%d" % h][:, zs], E["T"].F[:, 0:W].indirect(E["T"][RN][:, cols]), AF.Copy))
+                if (m, j) in S_GATHER:
+                    a(256 * 1.5 + 60, ["F", ("RN", h, t)], [("Z", h, m, j)], lambda E, z2=z2, cols=cols: E["g"].scalar.activation(
+                        E["T"][Z][:, z2], E["T"].F[:, D0:KW].indirect(E["T"][RN][:, cols]), AF.Copy))
                 else:
-                    v(256 * 1.5 + 50, ["F", ("XT", h), ("RN", h, t)], [("Z", h, m, j)], lambda E, zs=z2, cols=cols: E["g"].vector.tensor_copy(
-                        E["T"]["Z%d" % h][:, zs], E["T"].F[:, 0:W].indirect(E["T"][RN][:, cols])))
-            mm(512, [("QT", h)] + ERall, [("bank", XB), ("xq", h, m)], [
-                (lambda T, XB=XB: T[XB][:], lambda T: T["QT%d" % h][0:LH, :], lambda T, zs=zs: T.ER[0:LH, zs], True, False)])
-            mm(512, ["NI", ("Z", h, m, 0), ("Z", h, m, 1), ("xq", h, m)], [("bank", XB), ("xd", h, m)], [
-                (lambda T, XB=XB: T[XB][:], lambda T: T.NI[:], lambda T, zs=zs: T["Z%d" % h][:, zs], False, True)])
-            act(512, [("bank", XB), ("xd", h, m)], [("AX", h, m)], lambda T, m=m: T["AX%d" % h][:, 2 * m:2 * m + 2, :], lambda T, XB=XB: T[XB][:], AF.Abs)
-        for c2 in range(2):
-            mm(512, [("XT", h)] + [("SWM", i) for i in range(4)], [("bank", QD), ("KN", h, c2)], [
-                (lambda T, c2=c2: T[QD][:, 16 + c2:16 + C:2, :], lambda T, g2=g2, c2=c2: T.SWM[:, 2 * g2 + c2, :],
-                 lambda T, g2=g2: T["XT%d" % h][:, :, 16 * g2:16 * g2 + 16], g2 == 0, g2 == 1) for g2 in range(2)])
+                    v(256 * 1.5 + 50, ["F", ("RN", h, t)], [("Z", h, m, j)], lambda E, z2=z2, cols=cols: E["g"].vector.tensor_copy(
+                        E["T"][Z][:, z2], E["T"].F[:, D0:KW].indirect(E["T"][RN][:, cols])))
+            mm(512, [("QT", h)] + ERall, [("bank", X), ("xq", h, m)], [
+                (whole(X), lambda T: T["QT%d" % h][0:LH, :], lambda T, zs=zs: T.ER[0:LH, zs], True, False)])
+            mm(512, ["NI", ("Z", h, m, 0), ("Z", h, m, 1), ("xq", h, m)], [("bank", X), ("xd", h, m)], [
+                (whole(X), whole("NI"), lambda T, zs=zs: T[Z][:, zs], False, True)])
+            act(512, [("bank", X), ("xd", h, m)], [("AX", h, m)], lambda T, m=m: T[AX][:, 2 * m:2 * m + 2, :], whole(X), AF.Abs)
         for q in range(C // 4):
             for r4 in range(4):
                 mm(4 * 64, [("AX", h, 2 * q), ("AX", h, 2 * q + 1)] + LRall, [("bank", QD), ("D", h, q, r4)], [
                     (lambda T, q=q: T[QD][:, 4 * q:4 * q + 4, :], lambda T, r=r: T.LR[:, r, :],
-                     lambda T, r=r, q=q: T["AX%d" % h][:, 4 * q:4 * q + 4, 16 * r:16 * r + 16], r == 0, r == 15) for r in range(4 * r4, 4 * r4 + 4)])
+                     lambda T, r=r, q=q: T[AX][:, 4 * q:4 * q + 4, 16 * r:16 * r + 16], r == 0, r == 15) for r in range(4 * r4, 4 * r4 + 4)])
 
     def mid(t, h):
         HS = str(h)
-        RX, TX, MM, SM, LTB = "RX" + HS, "TX" + HS, "MM" + HS, "SM" + HS, "LT" + HS
-        x0, n0 = LH * t, 2 * LH * t
-        QC, QD, CL, RN = "QC" + HS, "QD" + HS, "CL" + HS, "RN" + HS
-        tl = lambda T: T["TL" + HS][:]
+        RX, RL, TX, CL, MM, SM, LTB, QC, QD = (x + HS for x in ("RX", "RL", "TX", "CL", "MM", "SM", "LT", "QC", "QD"))
+        x0, q0 = LH * t, h * 3 * LH
+        own = lambda x: whole(x + HS)
+        slot = lambda x: (lambda T: T[x + HS][:, x0:x0 + LH])
+        tn = lambda i: (lambda T: T["TN" + HS][:, 2 * x0 + i * LH:2 * x0 + (i + 1) * LH])
         sm = lambda i: (lambda T: T[SM][:, i * LH:(i + 1) * LH])
+        last = lambda i: (lambda T: T[SM][:, i * LH + 15:(i + 1) * LH:16])
         lt = lambda i: (lambda T: T[LTB][:, 8 * i:8 * i + C])
-        ol = lambda T: T["OL" + HS][:]
-        ex = lambda T: T.EX[:]
-        bank = lambda b: ("bank", b)
-        q0 = h * 3 * LH
+        by = lambda tab, lst: (lambda T: T[tab][:, 0:KW].indirect(T[lst + HS][:]))
+        ol, oi, ht, tl = own("OL"), own("OI"), own("HT"), own("TL")
         qs = lambda i: (lambda T: T[QC][:, i * LH:(i + 1) * LH])
-        st = lambda T: T.QU[:, q0:q0 + LH]
-        e0 = qs(2)
-        uu = lambda a_, b_: (lambda T: T.QU[:, q0 + LH * a_:q0 + LH * b_])
-        mk = lambda T: T[MM][:, 0:LH]
-        mo = lambda T: T[MM][:, LH:2 * LH]
-        tn = lambda T: T["TN" + HS][:, n0:n0 + LH]
-        dreg = [("D", h, q, r4) for q in range(C // 4) for r4 in range(4)]
-        ts(LH, [bank(QD)] + dreg + ["LM%d" % t], [("S1", h)], lambda T: T["S1" + HS][:], lambda T: T[QD][:, 0:C, :],
-           lambda T: T.LM[:, t:t + 1], None, A.max)
-        tt(LH // 2, [("S1", h), bank(QD), ("KN", h, 0), ("KN", h, 1)], [("S2", h)], lambda T: T["S2" + HS][:], lambda T: T["S1" + HS][:],
-           lambda T: T[QD][:, 16:16 + C, :], A.add)
-        v(LH, [("S2", h), "R2"], [("SC", h)], lambda E: E["g"].vector.tensor_tensor_scan(
-            E["T"]["SC" + HS][:], E["T"].R2[:], E["T"]["S2" + HS][:], 0.0, A.max, A.min))
+        qu = lambda i, j: (lambda T: T.QU[:, q0 + LH * i:q0 + LH * j])
+        st, e0 = qu(0, 1), qs(2)
+        mk, mo = lambda T: T[MM][:, 0:LH], lambda T: T[MM][:, LH:2 * LH]
+        bc, bd, bu = ("bank", QC), ("bank", QD), ("bank", "QU")
+        lm = lambda T: T.LM[:, t:t + 1]
+        ts(LH, [bd, "LM%d" % t] + [("D", h, q, r4) for q in range(C // 4) for r4 in range(4)], [("S1", h)], own("S1"),
+           lambda T: T[QD][:, 0:C, :], lm, None, A.max)
+        tt(LH // 2, [("S1", h), bd, ("KN", h)], [("S2", h)], own("S2"), own("S1"), lambda T: T[QD][:, 16:16 + C, :], A.add)
+        scan(LH, [("S2", h), "R2"], [("SC", h)], own("SC"), whole("R2"), own("S2"), 0.0, A.max, A.min)
         sc = lambda T: T["SC" + HS][:, 15:LH:16]
-        ts(C, [("SC", h)], [("OI", h)], lambda T: T["OI" + HS][:], sc, 2047, None, A.bitwise_and)
-        tc(C, [("OI", h)], [("OL", h)], ol, lambda T: T["OI" + HS][:])
+        ts(C, [("SC", h)], [("OI", h)], oi, sc, 4095, None, A.bitwise_and)
+        tc(C, [("OI", h)], [("OL", h)], ol, oi)
         OLr = [("OL", h)]
-        tt(LH, OLr + KTall + [("MK", h)], [("HT", h)], lambda T: T["HT" + HS][:], lambda T: T.KT[:, 0:W].indirect(ol(T)), mk, A.is_equal, True)
-        ht = lambda T: T["HT" + HS][:]
-        mm(LH, [("HT", h), "PW"], [bank(QC), ("S", h)], [(qs(0), lambda T: T.PW[:], ht, True, True)])
-        tt(LH, [("HT", h), ("MO", h)], [("sm", h, 0)], sm(0), ht, mo, A.mult)
-        ts(LH, [bank(QC), ("S", h), cpy(THR)], [("sm", h, 1)], sm(1), qs(0), co(THR), None, A.is_lt)
-        tt(LH, [("sm", h, 0), ("sm", h, 1)], [("sm", h, 2)], sm(2), sm(1), sm(0), A.mult)
-        mm(5 * LH, [("sm", h, 2), "BF", "IB", "OD"], [bank(QC), ("e", h)], [
-            (e0, lambda T: T.IB[:], lambda T: T.OD[:], True, False), (e0, lambda T: T.BF[:], sm(2), False, True)])
-        mm(LH, [("HT", h), "PSa", "PSb"], [bank(QC), ("Sp", h)], [(qs(1), lambda T: T.PS_[:], ht, True, True)])
-        v(LH, [bank(QC), ("e", h), "R2"], [("sm", h, 3)], lambda E: E["g"].vector.tensor_tensor_scan(
-            sm(3)(E["T"]), E["T"].R2[:], e0(E["T"]), 0.0, A.max, A.min))
-        ev = lambda T: T[SM][:, 3 * LH + 15:4 * LH:16]
-        tc(C, [("sm", h, 3)], [("EL", h)], lambda T: T["EL" + HS][:], ev)
+        tt(LH * 3 // 4 + 25, OLr + KTall + [("MK", h)], [("HT", h)], ht, by("KT", "OL"), mk, A.is_equal)
+        mm(LH, [("HT", h), "PW"], [bc, ("S", h)], [(qs(0), whole("PW"), ht, True, True)])
+        tt(LH // 2, [bc, ("S", h), ("HT", h)], [("sm", h, 1)], sm(1), qs(0), ht, A.is_lt)
+        tt(LH, [("MO", h), ("sm", h, 1)], [("sm", h, 2)], sm(2), sm(1), mo, A.mult)
+        mm(5 * LH, [("sm", h, 2), "BF", "IB", "OD"], [bc, ("e", h)], [
+            (e0, whole("IB"), whole("OD"), True, False), (e0, whole("BF"), sm(2), False, True)])
+        mm(LH, [("HT", h), "PSa"], [bc, ("Sp", h)], [(qs(1), whole("PS_"), ht, True, True)])
+        scan(LH, [bc, ("e", h), "R2"], [("sm", h, 3)], sm(3), whole("R2"), e0, 0.0, A.max, A.min)
+        ts(C, [("sm", h, 3)], [("EL", h)], own("EL"), last(3), float(D0 - U0), 0.0, A.add, A.max)
         if t < STEPS - 1:
-            tt(LH, OLr + ["F", ("RXq", h, t)], [("sm", h, 8)], sm(8), lambda T: T.F[:, 0:W].indirect(ol(T)), lambda T: T[RX][:, x0:x0 + LH], A.subtract, True)
-            act(LH, [("sm", h, 8)], [("TXq", h, t)], lambda T: T[TX][:, x0:x0 + LH], sm(8), AF.Abs)
-            op("g", 1.0, [("TXq", h, t)], [("sent", "x", h, t)], lambda E: E["send"]("x", t, h), "send")
-            op("net", TRANSIT, [("sent", "x", h, t)], [("RXq", h, t + 1)], None, ("ax", t + 1, h))
-        act(LH * 1.5, OLr + ["IDT"], [("TL", h)], tl, lambda T: T.IDT[:, 0:W].indirect(ol(T)))
+            tt(LH, OLr + ["F", "Fd", ("RXq", h, t)], [("sm", h, 8)], sm(8), by("F", "OL"), slot("RX"), A.subtract)
+            act(LH, [("sm", h, 8)], [("TXq", h, t)], slot("TX"), sm(8), AF.Abs)
+            op("g", ISSUE, [("TXq", h, t)], [("sent", "x", h, t)], lambda E: E["send"]("x", t, h), "send")
+            op("net", 0.0, [("sent", "x", h, t)], [("RXq", h, t + 1)], None, ("ax", t + 1, h))
+        act(LH * 1.5, OLr + ["IDT"], [("TL", h)], tl, by("IDT", "OL"))
         if t < STEPS - 1:
-            tc(LH, [("TL", h)], [("TNl", h, t)], lambda T: T["TN" + HS][:, n0 + LH:n0 + 2 * LH], tl)
-        ts(LH, [bank(QC), ("Sp", h)], [("sm", h, 4)], sm(4), qs(1), 0.0, None, A.is_le)
-        ts(LH, [bank(QC), ("Sp", h)], [("sm", h, 5)], sm(5), qs(1), 0.0, None, A.is_gt)
-        tt(LH, OLr + Kall + [("sm", h, 4)], [("sm", h, 6)], sm(6), lambda T: T.K[:, D0:KW].indirect(ol(T)), sm(4), A.mult, True)
-        tt(LH, [("EL", h), ("sm", h, 5)] + Kall, [("sm", h, 7)], sm(7), lambda T: T.K[:, 0:KW].indirect(T["EL" + HS][:]), sm(5), A.mult, True)
-        tt(LH, [("sm", h, 6), ("sm", h, 7)], [("TN", h, t)], tn, sm(7), sm(6), A.add)
-        op("g", 1.0, [("TN", h, t)] + ([("TNl", h, t)] if t < STEPS - 1 else []), [("sent", "n", h, t)], lambda E: E["send"]("n", t, h), "send")
-        op("net", TRANSIT, [("sent", "n", h, t)], [("RN", h, t + 1), ("RNl", h, t + 1)], None, ("an", t + 1, h))
+            tc(LH, [("TL", h)], [("TNl", h, t)], tn(1), tl)
+        ts(LH, [bc, ("Sp", h)], [("sm", h, 4)], sm(4), qs(1), 0.0, None, A.is_le)
+        ts(LH, [bc, ("Sp", h)], [("sm", h, 5)], sm(5), qs(1), 0.0, None, A.is_gt)
+        tt(LH, OLr + Kall + [("sm", h, 4)], [("sm", h, 6)], sm(6), by("K", "OL"), sm(4), A.mult)
+        tt(LH, [("EL", h), ("sm", h, 5)] + Kall, [("sm", h, 7)], sm(7), by("K", "EL"), sm(5), A.mult)
+        tt(LH, [("sm", h, 6), ("sm", h, 7)], [("TN", h, t)], tn(0), sm(7), sm(6), A.add)
+        op("g", ISSUE, [("TN", h, t)] + ([("TNl", h, t)] if t < STEPS - 1 else []), [("sent", "n", h, t)],
+           lambda E: E["send"]("n", t, h), "send")
+        op("net", 0.0, [("sent", "n", h, t)], [("RN", h, t + 1), ("RXl", h, t + 1)], None, ("an", t + 1, h))
         if t < STEPS - 1:
-            a(LH + 150, [bank(QC), ("S", h)], [("CN", t, h), ("junk", h)], lambda E: E["g"].scalar.activation(
-                E["T"]["SB" + HS][:], qs(0)(E["T"]), AF.Sign, accum_out=E["T"].CN[:, t * H + h:t * H + h + 1]))
-        ts(C, [("SC", h), "LI%d" % t], [("lt", h, 0)], lt(0), sc, lambda T: T.LM[:, 8 + t:9 + t], None, A.is_ge)
-        tt(LH, [("lt", h, 0), "EX", "DG"], [("ND", h)], lambda T: T["ND" + HS][:], lambda T: lt(0)(T).indirect(ex(T)), lambda T: T.DG[:], A.mult, True)
-        mm(2 * LH, [("ND", h), ("PI", t)], [bank("QU"), ("U", h)], [
-            (uu(1, 2), lambda T: T.PI[:, t, :], lambda T: T["ND" + HS][:], True, True),
-            (uu(2, 3), lambda T: T.PI[:, t, :], lambda T: T["ND" + HS][:], True, True)])
-        act(LH * 1.5, OLr + KTall, [("CLc", h)], lambda T: T[CL][:, 0:LH], lambda T: T.KT[:, 0:W].indirect(ol(T)))
+            a(LH + 150, [bc, ("S", h)], [("CN", t, h), ("junk", h)], lambda E: E["g"].scalar.activation(
+                own("SB")(E["T"]), qs(0)(E["T"]), AF.Sign, accum_out=E["T"].CN[:, t * H + h:t * H + h + 1]))
+        ts(C, [("SC", h), "LM%d" % t], [("lt", h, 0)], lt(0), sc, -SC, lm, A.add, A.is_ge)
+        tt(LH, [("lt", h, 0), "EX", "DG"], [("ND", h)], own("ND"), lambda T: lt(0)(T).indirect(T.EX[:]), whole("DG"), A.mult)
+        mm(2 * LH, [("ND", h), ("PI", t)], [bu, ("U", h)], [
+            (qu(i, i + 1), lambda T: T.PI[:, t, :], own("ND"), True, True) for i in (1, 2)])
+        act(LH * 1.5, OLr + KTall, [("CLc", h)], lambda T: T[CL][:, 0:LH], by("KT", "OL"))
         if t:
-            tc(LH, [("RNl", h, t)], [("CLl", h)], lambda T: T[CL][:, LH:2 * LH], lambda T: T[RN][:, n0 + LH:n0 + 2 * LH])
-        dd = lambda T: T["DD" + HS][:]
-        mall = lambda T: T[MM][:]
-        tt(2 * LH, [("CLc", h), ("CLl", h), ("MK", h), ("MO", h)], [("DD", h)], dd, lambda T: T[CL][:], mall, A.subtract)
-        tt(LH, [("DD", h), bank("QU"), ("U", h)], [("DD", h)], dd, dd, uu(1, 3), A.mult)
+            ts(LH, [("RXl", h, t)], [("CLl", h)], lambda T: T[CL][:, LH:2 * LH], lambda T: T["RN" + HS][:, 2 * x0 + LH:2 * x0 + 2 * LH], float(U0 - D0), None, A.add)
+        dd, mall = own("DD"), own("MM")
+        tt(2 * LH, [("CLc", h), ("CLl", h), ("MK", h), ("MO", h)], [("DD", h)], dd, own("CL"), mall, A.subtract)
+        tt(LH, [("DD", h), bu, ("U", h)], [("DD", h)], dd, dd, qu(1, 3), A.mult)
         tt(2 * LH, [("DD", h)], [("MK", h), ("MO", h)], mall, mall, dd, A.add)
-        ts(C, [("OI", h)], [("lt", h, 1)], lt(1), lambda T: T["OI" + HS][:], float(D0), None, A.add)
-        tt(LH, [("lt", h, 1), "EX", ("TL", h)], [("sb", h, 0)], sm(9), lambda T: lt(1)(T).indirect(ex(T)), tl, A.not_equal, True)
-        mm(2 * LH, [("HT", h), "PW", "IB", "NT"], [bank("QU"), ("St", h)], [
-            (st, lambda T: T.IB[:], lambda T: T.NT[:], True, False), (st, lambda T: T.PW[:], ht, False, True)])
-        ts(LH, [bank("QU"), ("St", h)], [("sm", h, 10)], sm(10), st, 0.5, None, A.is_lt)
-        tt(LH, [("sm", h, 10), ("sb", h, 0)], [("sm", h, 10)], sm(10), sm(10), sm(9), A.max)
-        v(LH, [("sm", h, 10), "R2"], [("sm", h, 11)], lambda E: E["g"].vector.tensor_tensor_scan(
-            sm(11)(E["T"]), E["T"].R2[:], sm(10)(E["T"]), 0.0, A.max, A.min))
-        ts(C, [("sm", h, 3)], [("lt", h, 2)], lt(2), ev, float(D0), None, A.is_ge)
-        tt(C, [("lt", h, 2), ("lt", h, 1)], [("lt", h, 3)], lt(3), lt(2), lt(1), A.mult)
-        tt(C, [("lt", h, 3), ("sm", h, 11)], [("lt", h, 4)], lt(4), lt(3), lambda T: T[SM][:, 11 * LH + 15:12 * LH:16], A.mult)
+        tt(LH, [("OI", h), "EX", ("TL", h)], [("sb", h, 0)], sm(9), lambda T: oi(T).indirect(T.EX[:]), tl, A.not_equal)
+        mm(2 * LH, [("HT", h), "PV", "IB", "NT"], [bu, ("St", h)], [
+            (st, whole("IB"), whole("NT"), True, False), (st, whole("PV"), ht, False, True)])
+        tt(LH // 2, [bu, ("St", h), ("sb", h, 0)], [("sm", h, 10)], sm(10), st, sm(9), A.is_le)
+        scan(LH, [("sm", h, 10), "R2"], [("sm", h, 11)], sm(11), whole("R2"), sm(10), 0.0, A.max, A.min)
+        tt(C, [("sm", h, 3), ("OI", h)], [("lt", h, 3)], lt(3), last(3), oi, A.min)
+        tt(C, [("lt", h, 3), ("sm", h, 11)], [("lt", h, 4)], lt(4), lt(3), last(11), A.mult)
         ts(C, [("lt", h, 4), "PT"], [("SL", h)], lambda T: T["SL" + HS][:, 0:2 * C:2], lt(4), pm, None, A.max)
 
     def scatters(t):
         for h in reversed(range(H)):
             for c in reversed(range(C)):
-                src = lambda T, h=h, c=c: T["TN%d" % h][:, 2 * LH * t + 16 * c:2 * LH * t + 16 * c + 16]
-                v(64, [("SL", h), ("TN", h, t)], Kall, lambda E, h=h, c=c, src=src: E["g"].vector.tensor_copy(
-                    E["T"].K[:, 0:KW].indirect(E["T"]["SL%d" % h][:, 2 * c:2 * c + 1]), src(E["T"])))
+                v(64, [("SL", h), ("TN", h, t)], Kall, lambda E, h=h, c=c: E["g"].vector.tensor_copy(
+                    E["T"].K[:, 0:KW].indirect(E["T"]["SL%d" % h][:, 2 * c:2 * c + 1]),
+                    E["T"]["TN%d" % h][:, 2 * LH * t + 16 * c:2 * LH * t + 16 * c + 16]))
 
     def count(t):
+        col = lambda n: (lambda T: T[n][:, t:t + 1])
         mm(256 * H, [("CN", t, h) for h in range(H)] + ["ON"], [("bank", "QU"), "cnt"], [
-            (lambda T: T.QU[:, 511:512], lambda T: T.ON[:], lambda T, h=h: T.CN[:, t * H + h:t * H + h + 1], h == 0, h == H - 1) for h in range(H)])
-        tc(1, [("bank", "QU"), "cnt"], [("CC", t)], lambda T: T.CC[:, t:t + 1], lambda T: T.QU[:, 511:512])
-        ts(1, [("CC", t)], [("CA", t)], lambda T: T.CA[:, t:t + 1], lambda T: T.CC[:, t:t + 1], 15, None, A.bitwise_and)
-        ts(1, [("CA", t)], ["LM%d" % (t + 1)], lambda T: T.LM[:, t + 1:t + 2], lambda T: T.CA[:, t:t + 1], 57.0, 32768.0, A.add, A.mult)
-        ts(1, [("CA", t)], ["LI%d" % (t + 1)], lambda T: T.LM[:, t + 9:t + 10], lambda T: T.CA[:, t:t + 1], 58.0, 32768.0, A.add, A.mult)
+            (lambda T: T.QU[:, 511:512], whole("ON"), lambda T, h=h: T.CN[:, t * H + h:t * H + h + 1], h == 0, h == H - 1) for h in range(H)])
+        tc(1, [("bank", "QU"), "cnt"], [("CC", t)], col("CC"), lambda T: T.QU[:, 511:512])
+        ts(1, [("CC", t)], [("CA", t)], col("CA"), col("CC"), 15, None, A.bitwise_and)
+        ts(1, [("CA", t)], ["LM%d" % (t + 1)], lambda T: T.LM[:, t + 1:t + 2], col("CA"), 57.0, SC, A.add, A.mult)
 
     setup_rest()
     for h in range(H):
@@ -392,6 +382,7 @@ def build():
             for b in range(4):
                 keytable(b)
             setup_late()
+    SETUP[0] = len(nodes)
     for t in range(STEPS):
         for h in range(H):
             if t:
@@ -400,23 +391,24 @@ def build():
         scatters(t)
         if t < STEPS - 1:
             count(t)
+    part = lambda n, h: (lambda T: T[n][:, h * LH:(h + 1) * LH])
     for h in range(H):
-        tc(LH, [("RN", h, STEPS)], [("YN", h)], lambda T, h=h: T.YN[:, h * LH:(h + 1) * LH], lambda T, h=h: T["RN%d" % h][:, 2 * STEPS * LH:(2 * STEPS + 1) * LH])
-    dma("dy", "oyn", [("YN", h) for h in range(H)], ["oyn"], lambda T: T.yn[:], lambda T: T.YN[:], 2.5)
+        tc(LH, [("RN", h, STEPS)], [("YN", h)], part("YN", h), lambda T, h=h: T["RN%d" % h][:, 2 * STEPS * LH:(2 * STEPS + 1) * LH])
+    dma("dy", "oyn", [("YN", h) for h in range(H)], ["oyn"], lambda T: T.yn[:], whole("YN"), 2.5)
     for h in range(H):
-        ts(LH, [("MO", h)], [("ym", h)], lambda T, h=h: T.YM[:, h * LH:(h + 1) * LH], lambda T, h=h: T["MM%d" % h][:, LH:2 * LH], 64.0, -64.0 * D0, A.mult, A.add)
-        tt(LH, [("ym", h), ("MK", h)], [("ym", h)], lambda T, h=h: T.YM[:, h * LH:(h + 1) * LH], lambda T, h=h: T.YM[:, h * LH:(h + 1) * LH],
-           lambda T, h=h: T["MM%d" % h][:, 0:LH], A.add)
-    dma("dy", "oym", [("ym", h) for h in range(H)], ["oym"], lambda T: T.ymu[:], lambda T: T.YM[:], 2.5)
+        ts(LH, [("MO", h)], [("ym", h)], part("YM", h), lambda T, h=h: T["MM%d" % h][:, LH:2 * LH], 64.0, -64.0 * U0, A.mult, A.add)
+        tt(LH, [("ym", h), ("MK", h)], [("ym", h)], part("YM", h), part("YM", h), lambda T, h=h: T["MM%d" % h][:, 0:LH], A.add)
+    dma("dy", "oym", [("ym", h) for h in range(H)], ["oym"], lambda T: T.ymu[:], whole("YM"), 2.5)
     kb = lambda b: (lambda T: T.K[:, D0 + 256 * b:D0 + 256 * b + 256])
     mm(4096, Kall + [("YI", b) for b in range(4)], [("bank", "X0")], [
         (lambda T: T.X0[:, 0, :], lambda T, b=b: T.YI[:, b, :], kb(b), b == 0, b == 3) for b in range(4)])
     for b in range(4, 8):
         act(256, Kall, [("YS", b)], lambda T, b=b: T.YS[:, b - 4, :], kb(b), AF.Copy, float(b + 1))
-    yd = lambda T: T.YD[:]
-    tt(256, [("YS", 4), ("YS", 5)], ["YD"], yd, lambda T: T.YS[:, 0, :], lambda T: T.YS[:, 1, :], A.add)
-    tt(256, ["YD", ("YS", 6)], ["YD"], yd, yd, lambda T: T.YS[:, 2, :], A.add)
-    tt(256, ["YD", ("YS", 7)], ["YD"], yd, yd, lambda T: T.YS[:, 3, :], A.add)
+    ys = lambda b: (lambda T: T.YS[:, b - 4, :])
+    yd = whole("YD")
+    tt(256, [("YS", 4), ("YS", 5)], ["YD"], yd, ys(4), ys(5), A.add)
+    tt(256, ["YD", ("YS", 6)], ["YD"], yd, yd, ys(6), A.add)
+    tt(256, ["YD", ("YS", 7)], ["YD"], yd, yd, ys(7), A.add)
     tt(256, ["YD", ("bank", "X0")], ["YD"], yd, yd, lambda T: T.X0[:, 0, :], A.add)
     dma("dy", "oyd", ["YD"], ["oyd"], lambda T: T.yd[:], yd, 2.5)
     return nodes
@@ -439,13 +431,10 @@ def plan():
                     need(j, True)
             acc.append(i)
         for k in R:
-            if k in bk:
-                if k in lastw:
-                    need(lastw[k], True)
-                continue
             if k in lastw:
                 need(lastw[k], True)
-            readers.setdefault(k, []).append(i)
+            if k not in bk:
+                readers.setdefault(k, []).append(i)
         for k in Wr:
             if k in bk:
                 if k in lastw and nodes[lastw[k]][0] == q:
@@ -462,84 +451,91 @@ def plan():
     for i in range(n):
         for j in deps[i]:
             succ[j].append(i)
-    prio = [0.0] * n
+
+    def first(i):
+        for k in nodes[i][3]:
+            if isinstance(k, tuple) and k[0] != "bank":
+                return (k[2] if k[0] == "sent" else k[1]) == 0 and k[0] in PATH
+        return i < SETUP[0]
+    prio, rank_ = [0.0] * n, [0.0] * n
     for i in reversed(range(n)):
-        prio[i] = nodes[i][1] + max([prio[j] + 0.08 for j in succ[i]] or [0.0])
-    left = [len(d) for d in deps]
-    fin, avail, order = [0.0] * n, {}, {}
-    ready = [i for i in range(n) if left[i] == 0]
-    seq = []
+        prio[i] = nodes[i][1] + (0.5 * (ON + OFF) if nodes[i][0] == "net" else 0.0) + max([prio[j] + LATX for j in succ[i]] or [0.0])
+        rank_[i] = prio[i] + (BON if first(i) else 0.0)
+    left = {(c, i): len(deps[i]) for c in range(2) for i in range(n)}
+    fin, avail, base, ready = {}, {}, {}, {}
+    seqs = [[], []]
 
-    def est(i):
-        q = nodes[i][0]
-        e = avail.get(q, 0.0)
+    def open_(c, i):
+        e = 0.0
         for j in deps[i]:
-            e = max(e, fin[j] + (0.1 if deps[i][j] else 0.0))
-        return e
-    while ready:
-        es = [(est(i), i) for i in ready]
-        lo = min(es)[0]
-        qb = nodes[min(es)[1]][0]
-        i = max((prio[i], -i) for e, i in es if nodes[i][0] == qb and e <= lo + 0.03)[1] * -1
-        e = est(i)
-        q = nodes[i][0]
-        ready.remove(i)
-        seq.append(i)
-        order.setdefault(q, []).append(i)
-        fin[i] = e + nodes[i][1]
-        avail[q] = e if q == "net" else (e + 0.1 if q in ("dy", "ds") else fin[i])
-        for j in succ[i]:
-            left[j] -= 1
-            if left[j] == 0:
-                ready.append(j)
-    real = {"v": "v", "a": "a", "ds": "a", "t": "t", "g": "g", "dy": "y"}
-    pos, cnt = {}, {}
-    for i in seq:
-        q, tag = nodes[i][0], nodes[i][5]
-        if q in CTR and tag != "send":
-            cnt[q] = cnt.get(q, 0) + 1
-            pos[i] = cnt[q]
-    known = {}
-    clock = {}
-    out = []
-    for i in seq:
-        q, tag = nodes[i][0], nodes[i][5]
-        if q == "net":
-            continue
-        rq = real[q]
-        kn = known.setdefault(rq, {})
-        waits = {}
-
-        for j in sorted(deps[i], key=lambda j: -pos.get(j, 0)):
-            if not deps[i][j]:
-                continue
-            qj, tj = nodes[j][0], nodes[j][5]
-            if qj == "net":
-                key, val = tj, 1
-            elif qj in ("dy", "ds"):
-                key, val = tj, 16
-            elif tj == "send":
-                continue
+            if nodes[i][0] == "net":
+                e = max(e, fin[1 - c, j] + (ON if c == 1 else OFF))
             else:
-                key, val = qj, pos[j]
-            if kn.get(key, 0) < val and waits.get(key, (0, None))[0] < val:
-                waits[key] = (val, j)
-        for key in list(waits):
-            val, j = waits[key]
-            for k2 in list(waits):
-                if k2 != key and k2 in waits and key in waits and clock.get(waits[k2][1], {}).get(key, 0) >= val:
-                    del waits[key]
-                    break
-        for key, (val, j) in waits.items():
-            kn[key] = max(kn.get(key, 0), val)
-            for k2, v2 in clock.get(j, {}).items():
-                kn[k2] = max(kn.get(k2, 0), v2)
-        c = dict(kn)
-        if i in pos:
-            c[q] = max(c.get(q, 0), pos[i])
-        clock[i] = c
-        out.append((rq, q, nodes[i][4], tag, [(k, w[0]) for k, w in waits.items()]))
-    return out, cnt, (max(fin), seq, fin)
+                e = max(e, fin[c, j] + ((LATS if nodes[j][0] == nodes[i][0] else LATX) if deps[i][j] else 0.0))
+        base[c, i] = e
+        ready.setdefault((c, nodes[i][0]), []).append(i)
+    for c in range(2):
+        for i in range(n):
+            if not deps[i]:
+                open_(c, i)
+    while True:
+        lo, key = None, None
+        for k, l in ready.items():
+            if l:
+                e = max(avail.get(k, 0.0), min(base[k[0], i] for i in l))
+                if lo is None or e < lo:
+                    lo, key = e, k
+        if key is None:
+            break
+        c, q = key
+        i = max((rank_[i], -i) for i in ready[key] if base[c, i] <= lo + WIN)[1] * -1
+        e = max(avail.get(key, 0.0), base[c, i])
+        ready[key].remove(i)
+        seqs[c].append(i)
+        fin[c, i] = e + nodes[i][1]
+        avail[key] = e if q == "net" else (e + 0.1 if q in ("dy", "ds") else fin[c, i])
+        for j in succ[i]:
+            c2 = 1 - c if nodes[j][0] == "net" else c
+            left[c2, j] -= 1
+            if left[c2, j] == 0:
+                open_(c2, j)
+    real = {"v": "v", "a": "a", "ds": "a", "t": "t", "g": "g", "dy": "y"}
+    res = []
+    for seq in seqs:
+        pos, cnt, known, clock, out = {}, {}, {}, {}, []
+        for i in seq:
+            q, tag = nodes[i][0], nodes[i][5]
+            if q in CTR and tag != "send":
+                cnt[q] = cnt.get(q, 0) + 1
+                pos[i] = cnt[q]
+        for i in seq:
+            q, tag = nodes[i][0], nodes[i][5]
+            if q == "net":
+                continue
+            kn = known.setdefault(real[q], {})
+            waits = {}
+            for j in sorted(deps[i], key=lambda j: -pos.get(j, 0)):
+                qj, tj = nodes[j][0], nodes[j][5]
+                if not deps[i][j] or tj == "send":
+                    continue
+                key, val = (tj, 1) if qj == "net" else ((tj, 16) if qj in ("dy", "ds") else (qj, pos[j]))
+                if kn.get(key, 0) < val and waits.get(key, (0, None))[0] < val:
+                    waits[key] = (val, j)
+            for key in list(waits):
+                for k2 in list(waits):
+                    if k2 != key and clock.get(waits[k2][1], {}).get(key, 0) >= waits[key][0]:
+                        del waits[key]
+                        break
+            for key, (val, j) in waits.items():
+                kn[key] = max(kn.get(key, 0), val)
+                for k2, v2 in clock.get(j, {}).items():
+                    kn[k2] = max(kn.get(k2, 0), v2)
+            clock[i] = dict(kn)
+            if i in pos:
+                clock[i][q] = max(clock[i].get(q, 0), pos[i])
+            out.append((real[q], q, nodes[i][4], tag, [(k, w[0]) for k, w in waits.items()]))
+        res.append((out, cnt, (max(fin.values()), seq, fin)))
+    return res
 
 
 CACHE = {}
@@ -549,29 +545,28 @@ def route(core, dst, cores, topo):
     if topo.may_write(core, dst):
         return None
     c = [x for x in topo.cores_of(core) if x not in cores and topo.may_write(x, dst)]
-    same = [x for x in c if topo.die(x) == topo.die(core)]
-    c = same or c
+    c = [x for x in c if topo.die(x) == topo.die(core)] or c
     return {"x": c[0], "n": c[-1]}
-
-
-def bits(m):
-    return bin(m).count("1")
 
 
 def rank_program(g, core, T, topo):
     cores = list(T.cores)
     rank = T.rank_of(core)
 
-    def remote(p, out, in_, sem, dst):
-        rid, pid = topo.addr(dst, core)
-        g.remote_dma(out, in_, T.sem[sem], T.sem.ls, pid, rid, topo.mask(core, dst))
-        return bits(topo.mask(core, dst))
-
-    WX, WN = LH, 2 * LH
-
     def piece(p, buf, k, t):
-        w = WX if p == "x" else WN
+        w = LH if p == "x" else 2 * LH
         return T[buf][:, k * w:k * w + (LH if t == STEPS - 1 else w)]
+
+    def message(p, t, h, dst, out, in_):
+        rid, pid = topo.addr(dst, core)
+        g.remote_dma(out, in_, T.sem["a%s%d_%d" % (p, t + 1, h)], T.sem.ls, pid, rid, topo.mask(core, dst))
+        return len(topo.engines(core, dst))
+
+    def landing(p, t, h):
+        return piece(p, "R%s%d" % (p.upper(), h), t + 1, t)
+
+    def handed(p, t, h):
+        return piece(p, "RY" + p.upper(), t * H + h, t)
 
     if rank is None:
         total = 0
@@ -585,32 +580,26 @@ def rank_program(g, core, T, topo):
         for t in range(STEPS):
             for h in range(H):
                 for p, src, dst in jobs:
-                    if p == "x" and t == STEPS - 1:
-                        continue
-                    k = t * H + h
-                    buf = piece(p, "RY" + p.upper(), k, t)
-                    out = piece(p, "R%s%d" % (p.upper(), h), t + 1, t)
-                    sem = "a%s%d_%d" % (p, t + 1, h)
-                    g.wait_ge(T.sem[sem], bits(topo.mask(src, core)))
-                    total += remote(p, out, buf, sem, dst)
+                    if p == "n" or t < STEPS - 1:
+                        g.wait_ge(T.sem["a%s%d_%d" % (p, t + 1, h)], len(topo.engines(src, core)))
+                        total += message(p, t, h, dst, landing(p, t, h), handed(p, t, h))
         if total:
             g.wait_ge(T.sem.ls, total)
         return
 
     if "p" not in CACHE:
         CACHE["p"] = plan()
-    prog, cnt, _ = CACHE["p"]
     nxt, prv = cores[(rank + 1) % N], cores[(rank - 1) % N]
     ro_out, ro_in = route(core, nxt, cores, topo), route(prv, core, cores, topo)
+    prog, cnt, _ = CACHE["p"][0 if ro_out is None else 1]
     tot = [0]
 
     def send(p, t, h):
         src = piece(p, "T%s%d" % (p.upper(), h), t, t)
-        sem = "a%s%d_%d" % (p, t + 1, h)
         if ro_out is None:
-            tot[0] += remote(p, piece(p, "R%s%d" % (p.upper(), h), t + 1, t), src, sem, nxt)
+            tot[0] += message(p, t, h, nxt, landing(p, t, h), src)
         else:
-            tot[0] += remote(p, piece(p, "RY" + p.upper(), t * H + h, t), src, sem, ro_out[p])
+            tot[0] += message(p, t, h, ro_out[p], handed(p, t, h), src)
 
     E = {"g": g, "T": T, "send": send}
     eng = {"v": g.vector, "a": g.scalar, "t": g.tensor, "g": g, "y": g.sync}
@@ -619,13 +608,12 @@ def rank_program(g, core, T, topo):
             if isinstance(key, tuple):
                 p, t, h = key
                 frm = prv if ro_in is None else ro_in[p[1]]
-                eng[rq].wait_ge(T.sem["%s%d_%d" % (p, t, h)], bits(topo.mask(frm, core)))
+                eng[rq].wait_ge(T.sem["%s%d_%d" % (p, t, h)], len(topo.engines(frm, core)))
             else:
                 eng[rq].wait_ge(T.sem[CTR[key] if key in CTR else key], val)
         i = fn(E)
-        if tag == "send":
-            continue
-        i.then_inc(T.sem[CTR[q]] if q in CTR else T.sem[tag], 1 if q in CTR else 16)
+        if tag != "send":
+            i.then_inc(T.sem[CTR[q]] if q in CTR else T.sem[tag], 1 if q in CTR else 16)
     for q in CTR:
         g.wait_ge(T.sem[CTR[q]], cnt[q])
     for n in DMAS:

from concourse.mybir import AluOpType, AxisListType, ActivationFunctionType

A = AluOpType
AF = ActivationFunctionType
N, STEPS, L, W = 8, 8, 128, 2048
H = 2
LH = L // H
C = LH // 16
NCH = LH // 32
D0 = 16
U0 = 4096
KW = D0 + W
BIG = 16777216.0
RND = 12582912.0
SC = 65536.0
S_GATHER = ((0, 0), (0, 1))
ON, OFF, LATX, LATS, BON, WIN = 5.0, 5.0, 0.1, 0.1, 0.0, 0.03
ISSUE = 1.0

SCRATCH = {
    "F": ("sbuf", [128, KW], "bfloat16"), "KI": ("sbuf", [128, W], "int32"), "K": ("sbuf", [128, KW], "float32"),
    "KT": ("sbuf", [128, KW], "bfloat16"), "IDT": ("sbuf", [128, KW], "float32"), "HI": ("sbuf", [128, W], "bfloat16"),
    "WQ": ("sbuf", [128, 4, 512], "float32"), "CI": ("sbuf", [128, L], "int32"), "LI": ("sbuf", [128, L], "int32"),
    "LF": ("sbuf", [128, L], "float32"), "MKB": ("sbuf", [128, L], "bfloat16"), "MOI": ("sbuf", [128, L], "int32"),
    "WI": ("sbuf", [128, 1], "int32"), "IM": ("sbuf", [128, 128], "float32"), "RI": ("sbuf", [128, 128], "float32"),
    "GI": ("sbuf", [128, 128], "float32"), "PC": ("sbuf", [128, 8], "int32"), "PA": ("sbuf", [128, 8], "int32"),
    "PB": ("sbuf", [128, 8], "int32"), "PT": ("sbuf", [128, 8], "float32"), "CO": ("sbuf", [128, 32], "float32"),
    "P2": ("sbuf", [128, 48], "float32"), "IF": ("sbuf", [128, 128], "float32"), "IB": ("sbuf", [128, 128], "bfloat16"),
    "NI": ("sbuf", [128, 128], "bfloat16"), "N64": ("sbuf", [128, 128], "bfloat16"), "BF": ("sbuf", [128, 128], "float32"),
    "RB": ("sbuf", [128, 128], "bfloat16"), "RF": ("sbuf", [128, 128], "float32"), "WC": ("sbuf", [128, 128], "bfloat16"),
    "B8": ("sbuf", [128, 128], "float32"), "T1": ("sbuf", [128, 128], "float32"), "T2": ("sbuf", [128, 128], "float32"),
    "T3": ("sbuf", [128, 128], "float32"), "LR": ("sbuf", [128, 16, 128], "bfloat16"), "PI": ("sbuf", [128, 8, 128], "bfloat16"),
    "PW": ("sbuf", [128, 128], "bfloat16"), "PS_": ("sbuf", [128, 128], "bfloat16"), "PV": ("sbuf", [128, 128], "bfloat16"),
    "OD": ("sbuf", [128, LH], "bfloat16"), "NT": ("sbuf", [128, LH], "bfloat16"), "DG": ("sbuf", [128, LH], "float32"),
    "R2": ("sbuf", [128, LH], "float32"), "ON": ("sbuf", [128, 128], "float32"), "EXI": ("sbuf", [128, C], "int32"),
    "EX": ("sbuf", [128, C], "uint16"), "ER": ("sbuf", [128, 16 * LH], "bfloat16"), "YI": ("sbuf", [128, 4, 128], "float32"),
    "CN": ("sbuf", [128, 32], "float32"), "CC": ("sbuf", [128, 16], "int32"), "CA": ("sbuf", [128, 16], "int32"),
    "LM": ("sbuf", [128, 16], "float32"), "YN": ("sbuf", [128, L], "float32"), "YM": ("sbuf", [128, L], "float32"),
    "YD": ("sbuf", [128, 256], "float32"), "YS": ("sbuf", [128, 4, 256], "float32"),
    "X0": ("psum", [128, 2, 256], "float32"), "X1": ("psum", [128, 2, 256], "float32"),
    "X2": ("psum", [128, 2, 256], "float32"), "QU": ("psum", [128, 512], "float32"),
    "RYX": ("sbuf", [128, 7 * L], "bfloat16"), "RYN": ("sbuf", [128, 16 * L], "uint16"),
}
for _h in range(H):
    SCRATCH["QD%d" % _h] = ("psum", [128, 32, 16], "float32")
    SCRATCH["QC%d" % _h] = ("psum", [128, 512], "float32")
    for _n, _s, _d in (("RN", [128, 27 * LH], "uint16"), ("RX", [128, 8 * LH], "bfloat16"), ("TN", [128, 24 * LH], "uint16"),
                       ("TX", [128, 8 * LH], "bfloat16"), ("TL", [128, LH], "float32"),
                       ("CL", [128, 2 * LH], "float32"), ("MM", [128, 2 * LH], "float32"), ("QT", [128, 128], "bfloat16"),
                       ("NF", [128, C, 32], "float32"), ("XT", [128, C, 32], "float32"), ("Z", [128, 16 * LH], "bfloat16"),
                       ("AX", [128, C, 256], "bfloat16"), ("S1", [128, C, 16], "float32"), ("S2", [128, LH], "float32"),
                       ("SC", [128, LH], "int32"), ("OI", [128, C], "int32"), ("OL", [128, C], "uint16"),
                       ("HT", [128, LH], "bfloat16"), ("SM", [128, 12 * LH], "float32"), ("SB", [128, LH], "bfloat16"),
                       ("LT", [128, 40], "float32"), ("EL", [128, C], "uint16"), ("SL", [128, 2 * C], "uint16"),
                       ("ND", [128, LH], "bfloat16"), ("DD", [128, 2 * LH], "float32"), ("FO", [128, LH], "bfloat16")):
        SCRATCH[_n + str(_h)] = ("sbuf", _s, _d)

DMAS = ["cand", "feat"] + ["want%d" % _h for _h in range(H)] + ["wts", "last", "mkey", "mobj", "kids", "oyn", "oym", "oyd"]
SEMAPHORES = ["v", "a", "t", "gq", "ls"] + ["d_" + n for n in DMAS] + \
    ["a%s%d_%d" % (p, t, h) for p in ("x", "n") for t in range(1, STEPS + (p == "n")) for h in range(H)]

CTR = {"v": "v", "a": "a", "t": "t", "g": "gq"}
PWC, DSG, KCC, SG1, SG2, PF, PG, B4, B5, QB = 1, 2, 3, 4, 5, 6, 7, 8, 9, 10
PATH = ("Z", "xq", "xd", "AX", "D", "KN", "XT", "NF", "S1", "S2", "SC", "OI", "OL", "HT", "S", "Sp", "sm", "e", "EL", "TN", "TXq",
        "qt", "QT", "sent", "FO", "qd")
SETUP = [0]


def build():
    nodes = []

    def op(q, us, R, Wr, fn, tag=None):
        nodes.append((q, us, list(R), list(Wr), fn, tag))

    def v(n, R, Wr, fn):
        op("v", 0.03 + max(64, n) * 0.00104, R, Wr, fn)

    def a(n, R, Wr, fn):
        op("a", 0.06 + max(64, n) * 0.00104, R, Wr, fn)

    def gq(n, Wr, fn):
        op("g", 0.15 + n * 0.0017, [], Wr, fn)

    def dma(q, name, R, Wr, out, in_, us=3.0):
        op(q, us, R, Wr, lambda E: (E["g"].sync if q == "dy" else E["g"].scalar).dma_start(out(E["T"]), in_(E["T"])), "d_" + name)

    def val(E, x):
        return x if isinstance(x, (int, float)) or x is None else x(E["T"])

    def ts(n, R, Wr, out, in0, s1, s2, o0, o1=None):
        if o1 is None:
            v(n, R, Wr, lambda E: E["g"].vector.tensor_scalar(out(E["T"]), in0(E["T"]), val(E, s1), None, o0))
        else:
            v(n, R, Wr, lambda E: E["g"].vector.tensor_scalar(out(E["T"]), in0(E["T"]), val(E, s1), val(E, s2), o0, o1))

    def tt(n, R, Wr, out, in0, in1, o):
        v(n * 2, R, Wr, lambda E: E["g"].vector.tensor_tensor(out(E["T"]), in0(E["T"]), in1(E["T"]), o))

    def scan(n, R, Wr, out, d0, d1, init, o0, o1):
        v(n, R, Wr, lambda E: E["g"].vector.tensor_tensor_scan(out(E["T"]), d0(E["T"]), d1(E["T"]), init, o0, o1))

    def tc(n, R, Wr, out, in_):
        v(n, R, Wr, lambda E: E["g"].vector.tensor_copy(out(E["T"]), in_(E["T"])))

    def ms(n, Wr, out, x):
        v(n, [], Wr, lambda E: E["g"].vector.memset(out(E["T"]), x))

    def act(n, R, Wr, out, in_, f=AF.Copy, scale=1.0):
        a(n, R, Wr, lambda E: E["g"].scalar.activation(out(E["T"]), in_(E["T"]), f, scale=scale))

    def mm(cyc, R, Wr, calls):
        def emit(E):
            i = None
            for out, l, r, st, sp in calls:
                i = E["g"].tensor.matmul(out(E["T"]), l(E["T"]), r(E["T"]), st, sp)
            return i
        op("t", 0.03 + cyc * 0.0007, R, Wr, emit)

    def co(i):
        return lambda T: T.CO[:, i:i + 1]

    def cpy(i):
        return "co%d" % i

    def whole(n):
        return lambda T: T[n][:]

    dma("dy", "cand", [], ["CI"], whole("CI"), lambda T: T.cand[:], 2.5)
    dma("ds", "wts", [], ["WI"], whole("WI"), lambda T: T.wts[:], 2.5)
    dma("dy", "feat", [], ["F"], lambda T: T.F[:, D0:KW], lambda T: T.feat[:], 5.0)
    for h in range(H):
        dma("ds", "want%d" % h, [], [("RXq", h, 0)], lambda T, h=h: T["RX%d" % h][:, 0:LH], lambda T, h=h: T.want[:, h * LH:(h + 1) * LH], 3.0)
    dma("dy", "last", [], ["LI"], lambda T: T.LI[0:8, :], lambda T: T.last[:], 5.5)
    dma("ds", "mkey", [], ["MKB"], whole("MKB"), lambda T: T.mkey[:], 5.5)
    dma("dy", "mobj", [], ["MOI"], whole("MOI"), lambda T: T.mobj[:], 6.0)
    dma("ds", "kids", [], ["KI"], whole("KI"), lambda T: T.kids[:], 8.0)

    def iota(n, name, pattern, base, cm, flag=True):
        if flag:
            gq(n, [name], lambda E: E["g"].iota(E["T"][name][:], pattern, base, cm, allow_small_or_imprecise_dtypes=True))
        else:
            gq(n, [name], lambda E: E["g"].iota(E["T"][name][:], pattern, base, cm))
    iota(8, "PC", [[5, 8]], 0, 1, False)
    iota(128, "IM", [[1, 128]], 0, 0)
    iota(128, "RI", [[0, 8], [1, 16]], 0, 0)
    iota(128, "GI", [[1, 8], [0, 16]], 0, 0)
    iota(C, "EXI", [[1, C]], 0, 0, False)
    iota(KW, "IDT", [[1, KW]], 0, 0)
    for h in range(H):
        tc(LH, ["CI"], [("RN", h, 0)], lambda T, h=h: T["RN%d" % h][:, 0:LH], lambda T, h=h: T.CI[:, h * LH:(h + 1) * LH])
    ts(8, ["PC"], ["PA"], whole("PA"), whole("PC"), 15, None, A.bitwise_and)
    tc(8, ["PA"], ["PT"], whole("PT"), whole("PA"))
    tc(1, ["PC"], [cpy(PF)], co(PF), lambda T: T.PC[:, 0:1])
    ts(1, ["PC"], ["PB0"], lambda T: T.PB[:, 0:1], lambda T: T.PC[:, 0:1], 4, None, A.arith_shift_right)
    tc(1, ["PB0"], [cpy(PG)], co(PG), lambda T: T.PB[:, 0:1])
    ts(1, ["PB0"], ["PB1"], lambda T: T.PB[:, 1:2], lambda T: T.PB[:, 0:1], 1, None, A.bitwise_and)
    tc(1, ["PB1"], [cpy(B4)], co(B4), lambda T: T.PB[:, 1:2])
    pm = lambda T: T.PT[:, 0:1]
    ts(128, ["IM", cpy(PF)], ["IF"], whole("IF"), whole("IM"), co(PF), None, A.is_equal)
    ts(128, ["IM", cpy(PF)], ["NI"], whole("NI"), whole("IM"), co(PF), -1.0, A.is_equal, A.mult)
    ts(128, ["IM", cpy(PF)], ["IB"], whole("IB"), whole("IM"), co(PF), None, A.is_equal)
    ts(128, ["GI", cpy(PG)], ["BF"], whole("BF"), whole("GI"), co(PG), None, A.is_equal)
    for k in range(16):
        act(LH, ["IB"], [("ER", k)], lambda T, k=k: T.ER[:, k:16 * LH:16], lambda T: T.IB[:, 0:LH])
    ERall = [("ER", k) for k in range(16)]
    ts(128, ["GI", cpy(PG)], ["RF"], whole("RF"), whole("GI"), co(PG), 100.0, A.not_equal, A.mult)
    tt(128, ["RF", "RI"], ["RB"], whole("RB"), whole("RF"), whole("RI"), A.add)
    for r in range(16):
        ts(64, ["RB"], [("LR", r)], lambda T, r=r: T.LR[:, r, :], whole("RB"), float(r), SC, A.is_equal, A.mult)
    LRall = [("LR", r) for r in range(16)]
    tc(1, ["WI"], [cpy(16)], co(16), whole("WI"))
    ts(128, ["BF", cpy(16)], ["WC"], whole("WC"), whole("BF"), co(16), None, A.mult)
    ts(128, ["IF"], ["N64"], whole("N64"), whole("IF"), -64.0, None, A.mult)
    ms(1, [cpy(QB)], co(QB), -63.0 / 128)

    def keytable(b):
        X = "X%d" % ((b + 1) % 3)
        xs = lambda j: (lambda T: T[X][:, j, :])
        fs = lambda j: (lambda T: T.F[:, D0 + 512 * b + 256 * j:D0 + 512 * b + 256 * j + 256])
        hs = lambda j: (lambda T: T.HI[:, 512 * b + 256 * j:512 * b + 256 * j + 256])
        wq = lambda j: (lambda T: T.WQ[:, b, 256 * j:256 * j + 256])
        mm(512, ["WC", "F"], [("bank", X)], [(xs(j), whole("WC"), fs(j), True, True) for j in range(2)])
        for j in range(2):
            a(256, [("bank", X), cpy(QB)], [("WQ", b, j)], lambda E, j=j: E["g"].scalar.activation(
                wq(j)(E["T"]), xs(j)(E["T"]), AF.Identity, bias=co(QB)(E["T"]), scale=1.0 / 64))
            ts(256, [("WQ", b, j)], [("HI", b, j)], hs(j), wq(j), RND, RND, A.add, A.subtract)
        mm(1024, ["WC", "F", "N64", ("HI", b, 0), ("HI", b, 1)], [("bank", X)], [
            c for j in range(2) for c in ((xs(j), whole("WC"), fs(j), True, False), (xs(j), whole("N64"), hs(j), False, True))])
        for j in range(2):
            act(256, [("bank", X)], [("KT", b, j)], lambda T, j=j: T.KT[:, D0 + 512 * b + 256 * j:D0 + 512 * b + 256 * j + 256], xs(j))
    KTall = ["KTd"] + [("KT", b, j) for b in range(4) for j in range(2)]

    def setup_rest():
        ms(1, ["P2a"], lambda T: T.P2[:, 0:16], 0.5)
        ms(1, ["P2b"], lambda T: T.P2[:, 16:32], 0.0)
        scan(16, ["P2a", "P2b"], ["P2c"], lambda T: T.P2[:, 32:48], lambda T: T.P2[:, 0:16], lambda T: T.P2[:, 16:32], 65536.0, A.mult, A.add)
        ts(64, ["RI", "PT"], ["DG"], whole("DG"), lambda T: T.RI[:, 0:LH], pm, None, A.is_equal)
        tt(16, ["P2c", "DG"], ["P2a"], lambda T: T.P2[:, 0:16], lambda T: T.P2[:, 32:48], lambda T: T.DG[:, 0:16], A.mult)
        v(16, ["P2a"], [cpy(PWC)], lambda E: E["g"].vector.tensor_reduce(
            E["T"].CO[:, PWC:PWC + 1], E["T"].P2[:, 0:16], AxisListType.X, A.add))
        ts(1, ["PT"], [cpy(KCC)], co(KCC), pm, 4096.0, float(D0), A.mult, A.add)
        ts(1, ["PT"], [cpy(17)], co(17), pm, 9.0, -2.0, A.is_ge, A.mult)
        ts(1, ["PT"], [cpy(18)], co(18), pm, 3.0, -2.0, A.is_ge, A.mult)
        ts(1, [cpy(17)], [cpy(19)], co(19), co(17), 1.0, None, A.add)
        tt(1, [cpy(18), cpy(17)], [cpy(20)], co(20), co(18), co(17), A.subtract)
        ts(1, [cpy(20)], [cpy(22)], co(22), co(20), 1.0, None, A.add)
        tt(1, [cpy(19), cpy(PWC)], [cpy(SG1)], co(SG1), co(19), co(PWC), A.mult)
        tt(1, [cpy(22), cpy(PWC)], [cpy(SG2)], co(SG2), co(22), co(PWC), A.mult)
        tt(1, [cpy(SG2), cpy(SG1)], [cpy(DSG)], co(DSG), co(SG2), co(SG1), A.subtract)
        ts(128, ["RI"], ["T1"], whole("T1"), whole("RI"), 0.0, 2.0, A.is_gt, A.mult)
        ts(128, ["RI"], ["T2"], whole("T2"), whole("RI"), 0.0, 2.0 ** -16, A.is_equal, A.mult)
        scan(128, ["T1", "T2"], ["T3"], whole("T3"), whole("T1"), whole("T2"), 0.0, A.mult, A.add)
        ts(128, ["BF", cpy(PWC)], ["T2"], whole("T2"), whole("BF"), co(PWC), None, A.mult)
        tt(128, ["T2", "T3"], ["PW"], whole("PW"), whole("T2"), whole("T3"), A.mult)
        ts(128, ["T2"], ["PV"], whole("PV"), whole("T2"), 2.0 ** -16, None, A.mult)
        ts(128, ["RI"], ["T1"], whole("T1"), whole("RI"), 8.0, None, A.is_ge)
        ts(128, ["T1", cpy(DSG), cpy(SG1)], ["T1"], whole("T1"), whole("T1"), co(DSG), co(SG1), A.mult, A.add)
        tt(128, ["T1", "BF"], ["PSa"], whole("PS_"), whole("T1"), whole("BF"), A.mult)
        ts(64, ["RI", "PT"], ["OD"], whole("OD"), lambda T: T.RI[:, 0:LH], pm, 8192.0, A.not_equal, A.mult)
        ts(64, ["RI", "PT"], ["NT"], whole("NT"), lambda T: T.RI[:, 0:LH], pm, -131072.0, A.is_ge, A.mult)
        tc(C, ["EXI"], ["EX"], whole("EX"), whole("EXI"))
        ts(64, ["RI"], ["R2"], whole("R2"), lambda T: T.RI[:, 0:LH], 0.0, BIG, A.is_equal, A.mult)
        ts(1, [cpy(B4)], [cpy(B5)], co(B5), co(B4), -1.0, 1.0, A.mult, A.add)

    def setup_late():
        for h in range(H):
            tc(LH, ["MKB"], [("MK", h)], lambda T, h=h: T["MM%d" % h][:, 0:LH], lambda T, h=h: T.MKB[:, h * LH:(h + 1) * LH])
            ts(LH, ["MOI"], [("MO", h)], lambda T, h=h: T["MM%d" % h][:, LH:2 * LH], lambda T, h=h: T.MOI[:, h * LH:(h + 1) * LH], float(U0), None, A.add)
        ms(16, ["Kd"], lambda T: T.K[:, 0:D0], 0.0)
        for b in range(4):
            tc(512, ["KI"], [("Kb", b)], lambda T, b=b: T.K[:, D0 + 512 * b:D0 + 512 * b + 512], lambda T, b=b: T.KI[:, 512 * b:512 * b + 512])
        for t in range(8):
            ts(128, ["RB", "PT"], [("PI", t)], lambda T, t=t: T.PI[:, t, :], whole("RB"), lambda T, t=t: T.PT[:, t:t + 1], None, A.is_equal)
        ms(128, ["ON"], whole("ON"), 1.0 / 16)
        tc(128, ["LI"], ["LF"], lambda T: T.LF[0:8, :], lambda T: T.LI[0:8, :])
        ts(128, ["GI", cpy(PF)], ["B8"], whole("B8"), whole("GI"), co(PF), None, A.is_equal)
        mm(512, ["B8", "LF"], [("bank", "QU")], [(lambda T: T.QU[:, 0:128], lambda T: T.B8[0:8, :], lambda T: T.LF[0:8, :], True, True)])
        for h in range(H):
            ts(LH, [("bank", "QU")], [("CLl", h)], lambda T, h=h: T["CL%d" % h][:, LH:2 * LH], lambda T, h=h: T.QU[:, h * LH:(h + 1) * LH], float(U0), None, A.add)
        for b in range(4):
            act(128, ["IF"], [("YI", b)], lambda T, b=b: T.YI[:, b, :], whole("IF"), AF.Copy, float(b + 1))

    ms(1, ["LM0"], lambda T: T.LM[:, 0:1], 57.0 * SC)
    ms(1, ["Fd"], lambda T: T.F[:, 0:D0], 0.0)
    ms(1, ["KTd"], lambda T: T.KT[:, 0:D0], 0.0)
    Kall = ["Kd"] + [("Kb", b) for b in range(4)] + ["K"]

    def front(t, h):
        RN, RX, QC, QD, Z, AX = ("%s%d" % (x, h) for x in ("RN", "RX", "QC", "QD", "Z", "AX"))
        n0 = 2 * LH * t
        mm(128, [("RXq", h, t), "IB"], [("bank", QC), ("qt", h)], [
            (lambda T: T[QC][0:LH, 384:512], lambda T: T[RX][:, LH * t:LH * t + LH], whole("IB"), True, True)])
        act(128, [("bank", QC), ("qt", h)], [("QT", h)], lambda T: T["QT%d" % h][0:LH, :], lambda T: T[QC][0:LH, 384:512])
        for g2 in range(2):
            ts(LH, [("RN", h, t), cpy(KCC), cpy(B5), cpy(B4)], [("NF", h, g2)], lambda T, g2=g2: T["NF%d" % h][:, :, 16 * g2:16 * g2 + 16],
               lambda T: T[RN][:, n0:n0 + LH], co(KCC), co(B4 if g2 else B5), A.add, A.mult)

        def turn(E):
            i = None
            for c in range(C):
                i = E["g"].vector.transpose(E["T"]["XT%d" % h][:, c, :], E["T"]["NF%d" % h][:, c, :])
            return i
        v(64 * C, [("NF", h, 0), ("NF", h, 1)], [("XT", h)], turn)
        tt(LH, [("XT", h)], [("bank", QD), ("KN", h)], lambda T: T[QD][:, 16:16 + C, :], lambda T: T["XT%d" % h][:, :, 0:16],
           lambda T: T["XT%d" % h][:, :, 16:32], A.add)
        for m in range(NCH):
            zs = slice(512 * m, 512 * m + 512)
            X = "X%d" % ((h * NCH + m) % 3)
            for j in range(2):
                cols = slice(n0 + 32 * m + 16 * j, n0 + 32 * m + 16 * j + 16)
                z2 = slice(512 * m + 256 * j, 512 * m + 256 * j + 256)
                if (m, j) in S_GATHER:
                    a(256 * 1.5 + 60, ["F", ("RN", h, t)], [("Z", h, m, j)], lambda E, z2=z2, cols=cols: E["g"].scalar.activation(
                        E["T"][Z][:, z2], E["T"].F[:, D0:KW].indirect(E["T"][RN][:, cols]), AF.Copy))
                else:
                    v(256 * 1.5 + 50, ["F", ("RN", h, t)], [("Z", h, m, j)], lambda E, z2=z2, cols=cols: E["g"].vector.tensor_copy(
                        E["T"][Z][:, z2], E["T"].F[:, D0:KW].indirect(E["T"][RN][:, cols])))
            mm(512, [("QT", h)] + ERall, [("bank", X), ("xq", h, m)], [
                (whole(X), lambda T: T["QT%d" % h][0:LH, :], lambda T, zs=zs: T.ER[0:LH, zs], True, False)])
            mm(512, ["NI", ("Z", h, m, 0), ("Z", h, m, 1), ("xq", h, m)], [("bank", X), ("xd", h, m)], [
                (whole(X), whole("NI"), lambda T, zs=zs: T[Z][:, zs], False, True)])
            act(512, [("bank", X), ("xd", h, m)], [("AX", h, m)], lambda T, m=m: T[AX][:, 2 * m:2 * m + 2, :], whole(X), AF.Abs)
        for q in range(C // 4):
            for r4 in range(4):
                mm(4 * 64, [("AX", h, 2 * q), ("AX", h, 2 * q + 1)] + LRall, [("bank", QD), ("D", h, q, r4)], [
                    (lambda T, q=q: T[QD][:, 4 * q:4 * q + 4, :], lambda T, r=r: T.LR[:, r, :],
                     lambda T, r=r, q=q: T[AX][:, 4 * q:4 * q + 4, 16 * r:16 * r + 16], r == 0, r == 15) for r in range(4 * r4, 4 * r4 + 4)])

    def mid(t, h):
        HS = str(h)
        RX, RL, TX, CL, MM, SM, LTB, QC, QD = (x + HS for x in ("RX", "RL", "TX", "CL", "MM", "SM", "LT", "QC", "QD"))
        x0, q0 = LH * t, h * 3 * LH
        own = lambda x: whole(x + HS)
        slot = lambda x: (lambda T: T[x + HS][:, x0:x0 + LH])
        tn = lambda i: (lambda T: T["TN" + HS][:, 2 * x0 + i * LH:2 * x0 + (i + 1) * LH])
        sm = lambda i: (lambda T: T[SM][:, i * LH:(i + 1) * LH])
        last = lambda i: (lambda T: T[SM][:, i * LH + 15:(i + 1) * LH:16])
        lt = lambda i: (lambda T: T[LTB][:, 8 * i:8 * i + C])
        by = lambda tab, lst: (lambda T: T[tab][:, 0:KW].indirect(T[lst + HS][:]))
        ol, oi, ht, tl = own("OL"), own("OI"), own("HT"), own("TL")
        qs = lambda i: (lambda T: T[QC][:, i * LH:(i + 1) * LH])
        qu = lambda i, j: (lambda T: T.QU[:, q0 + LH * i:q0 + LH * j])
        st, e0 = qu(0, 1), qs(2)
        mk, mo = lambda T: T[MM][:, 0:LH], lambda T: T[MM][:, LH:2 * LH]
        bc, bd, bu = ("bank", QC), ("bank", QD), ("bank", "QU")
        lm = lambda T: T.LM[:, t:t + 1]
        ts(LH, [bd, "LM%d" % t] + [("D", h, q, r4) for q in range(C // 4) for r4 in range(4)], [("S1", h)], own("S1"),
           lambda T: T[QD][:, 0:C, :], lm, None, A.max)
        tt(LH // 2, [("S1", h), bd, ("KN", h)], [("S2", h)], own("S2"), own("S1"), lambda T: T[QD][:, 16:16 + C, :], A.add)
        scan(LH, [("S2", h), "R2"], [("SC", h)], own("SC"), whole("R2"), own("S2"), 0.0, A.max, A.min)
        sc = lambda T: T["SC" + HS][:, 15:LH:16]
        ts(C, [("SC", h)], [("OI", h)], oi, sc, 4095, None, A.bitwise_and)
        tc(C, [("OI", h)], [("OL", h)], ol, oi)
        OLr = [("OL", h)]
        tt(LH * 3 // 4 + 25, OLr + KTall + [("MK", h)], [("HT", h)], ht, by("KT", "OL"), mk, A.is_equal)
        mm(LH, [("HT", h), "PW"], [bc, ("S", h)], [(qs(0), whole("PW"), ht, True, True)])
        tt(LH // 2, [bc, ("S", h), ("HT", h)], [("sm", h, 1)], sm(1), qs(0), ht, A.is_lt)
        tt(LH, [("MO", h), ("sm", h, 1)], [("sm", h, 2)], sm(2), sm(1), mo, A.mult)
        mm(5 * LH, [("sm", h, 2), "BF", "IB", "OD"], [bc, ("e", h)], [
            (e0, whole("IB"), whole("OD"), True, False), (e0, whole("BF"), sm(2), False, True)])
        mm(LH, [("HT", h), "PSa"], [bc, ("Sp", h)], [(qs(1), whole("PS_"), ht, True, True)])
        scan(LH, [bc, ("e", h), "R2"], [("sm", h, 3)], sm(3), whole("R2"), e0, 0.0, A.max, A.min)
        ts(C, [("sm", h, 3)], [("EL", h)], own("EL"), last(3), float(D0 - U0), 0.0, A.add, A.max)
        if t < STEPS - 1:
            tt(LH, OLr + ["F", "Fd", ("RXq", h, t)], [("sm", h, 8)], sm(8), by("F", "OL"), slot("RX"), A.subtract)
            act(LH, [("sm", h, 8)], [("TXq", h, t)], slot("TX"), sm(8), AF.Abs)
            op("g", ISSUE, [("TXq", h, t)], [("sent", "x", h, t)], lambda E: E["send"]("x", t, h), "send")
            op("net", 0.0, [("sent", "x", h, t)], [("RXq", h, t + 1)], None, ("ax", t + 1, h))
        act(LH * 1.5, OLr + ["IDT"], [("TL", h)], tl, by("IDT", "OL"))
        if t < STEPS - 1:
            tc(LH, [("TL", h)], [("TNl", h, t)], tn(1), tl)
        ts(LH, [bc, ("Sp", h)], [("sm", h, 4)], sm(4), qs(1), 0.0, None, A.is_le)
        ts(LH, [bc, ("Sp", h)], [("sm", h, 5)], sm(5), qs(1), 0.0, None, A.is_gt)
        tt(LH, OLr + Kall + [("sm", h, 4)], [("sm", h, 6)], sm(6), by("K", "OL"), sm(4), A.mult)
        tt(LH, [("EL", h), ("sm", h, 5)] + Kall, [("sm", h, 7)], sm(7), by("K", "EL"), sm(5), A.mult)
        tt(LH, [("sm", h, 6), ("sm", h, 7)], [("TN", h, t)], tn(0), sm(7), sm(6), A.add)
        op("g", ISSUE, [("TN", h, t)] + ([("TNl", h, t)] if t < STEPS - 1 else []), [("sent", "n", h, t)],
           lambda E: E["send"]("n", t, h), "send")
        op("net", 0.0, [("sent", "n", h, t)], [("RN", h, t + 1), ("RXl", h, t + 1)], None, ("an", t + 1, h))
        if t < STEPS - 1:
            a(LH + 150, [bc, ("S", h)], [("CN", t, h), ("junk", h)], lambda E: E["g"].scalar.activation(
                own("SB")(E["T"]), qs(0)(E["T"]), AF.Sign, accum_out=E["T"].CN[:, t * H + h:t * H + h + 1]))
        ts(C, [("SC", h), "LM%d" % t], [("lt", h, 0)], lt(0), sc, -SC, lm, A.add, A.is_ge)
        tt(LH, [("lt", h, 0), "EX", "DG"], [("ND", h)], own("ND"), lambda T: lt(0)(T).indirect(T.EX[:]), whole("DG"), A.mult)
        mm(2 * LH, [("ND", h), ("PI", t)], [bu, ("U", h)], [
            (qu(i, i + 1), lambda T: T.PI[:, t, :], own("ND"), True, True) for i in (1, 2)])
        act(LH * 1.5, OLr + KTall, [("CLc", h)], lambda T: T[CL][:, 0:LH], by("KT", "OL"))
        if t:
            ts(LH, [("RXl", h, t)], [("CLl", h)], lambda T: T[CL][:, LH:2 * LH], lambda T: T["RN" + HS][:, 2 * x0 + LH:2 * x0 + 2 * LH], float(U0 - D0), None, A.add)
        dd, mall = own("DD"), own("MM")
        tt(2 * LH, [("CLc", h), ("CLl", h), ("MK", h), ("MO", h)], [("DD", h)], dd, own("CL"), mall, A.subtract)
        tt(LH, [("DD", h), bu, ("U", h)], [("DD", h)], dd, dd, qu(1, 3), A.mult)
        tt(2 * LH, [("DD", h)], [("MK", h), ("MO", h)], mall, mall, dd, A.add)
        tt(LH, [("OI", h), "EX", ("TL", h)], [("sb", h, 0)], sm(9), lambda T: oi(T).indirect(T.EX[:]), tl, A.not_equal)
        mm(2 * LH, [("HT", h), "PV", "IB", "NT"], [bu, ("St", h)], [
            (st, whole("IB"), whole("NT"), True, False), (st, whole("PV"), ht, False, True)])
        tt(LH // 2, [bu, ("St", h), ("sb", h, 0)], [("sm", h, 10)], sm(10), st, sm(9), A.is_le)
        scan(LH, [("sm", h, 10), "R2"], [("sm", h, 11)], sm(11), whole("R2"), sm(10), 0.0, A.max, A.min)
        tt(C, [("sm", h, 3), ("OI", h)], [("lt", h, 3)], lt(3), last(3), oi, A.min)
        tt(C, [("lt", h, 3), ("sm", h, 11)], [("lt", h, 4)], lt(4), lt(3), last(11), A.mult)
        ts(C, [("lt", h, 4), "PT"], [("SL", h)], lambda T: T["SL" + HS][:, 0:2 * C:2], lt(4), pm, None, A.max)

    def scatters(t):
        for h in reversed(range(H)):
            for c in reversed(range(C)):
                v(64, [("SL", h), ("TN", h, t)], Kall, lambda E, h=h, c=c: E["g"].vector.tensor_copy(
                    E["T"].K[:, 0:KW].indirect(E["T"]["SL%d" % h][:, 2 * c:2 * c + 1]),
                    E["T"]["TN%d" % h][:, 2 * LH * t + 16 * c:2 * LH * t + 16 * c + 16]))

    def count(t):
        col = lambda n: (lambda T: T[n][:, t:t + 1])
        mm(256 * H, [("CN", t, h) for h in range(H)] + ["ON"], [("bank", "QU"), "cnt"], [
            (lambda T: T.QU[:, 511:512], whole("ON"), lambda T, h=h: T.CN[:, t * H + h:t * H + h + 1], h == 0, h == H - 1) for h in range(H)])
        tc(1, [("bank", "QU"), "cnt"], [("CC", t)], col("CC"), lambda T: T.QU[:, 511:512])
        ts(1, [("CC", t)], [("CA", t)], col("CA"), col("CC"), 15, None, A.bitwise_and)
        ts(1, [("CA", t)], ["LM%d" % (t + 1)], lambda T: T.LM[:, t + 1:t + 2], col("CA"), 57.0, SC, A.add, A.mult)

    setup_rest()
    for h in range(H):
        front(0, h)
        if h == 0:
            for b in range(4):
                keytable(b)
            setup_late()
    SETUP[0] = len(nodes)
    for t in range(STEPS):
        for h in range(H):
            if t:
                front(t, h)
            mid(t, h)
        scatters(t)
        if t < STEPS - 1:
            count(t)
    part = lambda n, h: (lambda T: T[n][:, h * LH:(h + 1) * LH])
    for h in range(H):
        tc(LH, [("RN", h, STEPS)], [("YN", h)], part("YN", h), lambda T, h=h: T["RN%d" % h][:, 2 * STEPS * LH:(2 * STEPS + 1) * LH])
    dma("dy", "oyn", [("YN", h) for h in range(H)], ["oyn"], lambda T: T.yn[:], whole("YN"), 2.5)
    for h in range(H):
        ts(LH, [("MO", h)], [("ym", h)], part("YM", h), lambda T, h=h: T["MM%d" % h][:, LH:2 * LH], 64.0, -64.0 * U0, A.mult, A.add)
        tt(LH, [("ym", h), ("MK", h)], [("ym", h)], part("YM", h), part("YM", h), lambda T, h=h: T["MM%d" % h][:, 0:LH], A.add)
    dma("dy", "oym", [("ym", h) for h in range(H)], ["oym"], lambda T: T.ymu[:], whole("YM"), 2.5)
    kb = lambda b: (lambda T: T.K[:, D0 + 256 * b:D0 + 256 * b + 256])
    mm(4096, Kall + [("YI", b) for b in range(4)], [("bank", "X0")], [
        (lambda T: T.X0[:, 0, :], lambda T, b=b: T.YI[:, b, :], kb(b), b == 0, b == 3) for b in range(4)])
    for b in range(4, 8):
        act(256, Kall, [("YS", b)], lambda T, b=b: T.YS[:, b - 4, :], kb(b), AF.Copy, float(b + 1))
    ys = lambda b: (lambda T: T.YS[:, b - 4, :])
    yd = whole("YD")
    tt(256, [("YS", 4), ("YS", 5)], ["YD"], yd, ys(4), ys(5), A.add)
    tt(256, ["YD", ("YS", 6)], ["YD"], yd, yd, ys(6), A.add)
    tt(256, ["YD", ("YS", 7)], ["YD"], yd, yd, ys(7), A.add)
    tt(256, ["YD", ("bank", "X0")], ["YD"], yd, yd, lambda T: T.X0[:, 0, :], A.add)
    dma("dy", "oyd", ["YD"], ["oyd"], lambda T: T.yd[:], yd, 2.5)
    return nodes


def plan():
    nodes = build()
    n = len(nodes)
    deps = [dict() for _ in range(n)]
    lastw, readers, banks = {}, {}, {}
    for i, (q, us, R, Wr, fn, tag) in enumerate(nodes):
        def need(j, hard):
            if j != i:
                deps[i][j] = deps[i].get(j, False) or hard
        bk = set(k for k in R + Wr if isinstance(k, tuple) and k[0] == "bank")
        for k in bk:
            acc = banks.setdefault(k, [])
            for j in acc:
                if nodes[j][0] != q:
                    need(j, True)
            acc.append(i)
        for k in R:
            if k in lastw:
                need(lastw[k], True)
            if k not in bk:
                readers.setdefault(k, []).append(i)
        for k in Wr:
            if k in bk:
                if k in lastw and nodes[lastw[k]][0] == q:
                    need(lastw[k], q != "t")
                lastw[k] = i
                continue
            if k in lastw:
                need(lastw[k], True)
            for j in readers.get(k, []):
                need(j, nodes[j][0] != q)
            readers[k] = []
            lastw[k] = i
    succ = [[] for _ in range(n)]
    for i in range(n):
        for j in deps[i]:
            succ[j].append(i)

    def first(i):
        for k in nodes[i][3]:
            if isinstance(k, tuple) and k[0] != "bank":
                return (k[2] if k[0] == "sent" else k[1]) == 0 and k[0] in PATH
        return i < SETUP[0]
    prio, rank_ = [0.0] * n, [0.0] * n
    for i in reversed(range(n)):
        prio[i] = nodes[i][1] + (0.5 * (ON + OFF) if nodes[i][0] == "net" else 0.0) + max([prio[j] + LATX for j in succ[i]] or [0.0])
        rank_[i] = prio[i] + (BON if first(i) else 0.0)
    left = {(c, i): len(deps[i]) for c in range(2) for i in range(n)}
    fin, avail, base, ready = {}, {}, {}, {}
    seqs = [[], []]

    def open_(c, i):
        e = 0.0
        for j in deps[i]:
            if nodes[i][0] == "net":
                e = max(e, fin[1 - c, j] + (ON if c == 1 else OFF))
            else:
                e = max(e, fin[c, j] + ((LATS if nodes[j][0] == nodes[i][0] else LATX) if deps[i][j] else 0.0))
        base[c, i] = e
        ready.setdefault((c, nodes[i][0]), []).append(i)
    for c in range(2):
        for i in range(n):
            if not deps[i]:
                open_(c, i)
    while True:
        lo, key = None, None
        for k, l in ready.items():
            if l:
                e = max(avail.get(k, 0.0), min(base[k[0], i] for i in l))
                if lo is None or e < lo:
                    lo, key = e, k
        if key is None:
            break
        c, q = key
        i = max((rank_[i], -i) for i in ready[key] if base[c, i] <= lo + WIN)[1] * -1
        e = max(avail.get(key, 0.0), base[c, i])
        ready[key].remove(i)
        seqs[c].append(i)
        fin[c, i] = e + nodes[i][1]
        avail[key] = e if q == "net" else (e + 0.1 if q in ("dy", "ds") else fin[c, i])
        for j in succ[i]:
            c2 = 1 - c if nodes[j][0] == "net" else c
            left[c2, j] -= 1
            if left[c2, j] == 0:
                open_(c2, j)
    real = {"v": "v", "a": "a", "ds": "a", "t": "t", "g": "g", "dy": "y"}
    res = []
    for seq in seqs:
        pos, cnt, known, clock, out = {}, {}, {}, {}, []
        for i in seq:
            q, tag = nodes[i][0], nodes[i][5]
            if q in CTR and tag != "send":
                cnt[q] = cnt.get(q, 0) + 1
                pos[i] = cnt[q]
        for i in seq:
            q, tag = nodes[i][0], nodes[i][5]
            if q == "net":
                continue
            kn = known.setdefault(real[q], {})
            waits = {}
            for j in sorted(deps[i], key=lambda j: -pos.get(j, 0)):
                qj, tj = nodes[j][0], nodes[j][5]
                if not deps[i][j] or tj == "send":
                    continue
                key, val = (tj, 1) if qj == "net" else ((tj, 16) if qj in ("dy", "ds") else (qj, pos[j]))
                if kn.get(key, 0) < val and waits.get(key, (0, None))[0] < val:
                    waits[key] = (val, j)
            for key in list(waits):
                for k2 in list(waits):
                    if k2 != key and clock.get(waits[k2][1], {}).get(key, 0) >= waits[key][0]:
                        del waits[key]
                        break
            for key, (val, j) in waits.items():
                kn[key] = max(kn.get(key, 0), val)
                for k2, v2 in clock.get(j, {}).items():
                    kn[k2] = max(kn.get(k2, 0), v2)
            clock[i] = dict(kn)
            if i in pos:
                clock[i][q] = max(clock[i].get(q, 0), pos[i])
            out.append((real[q], q, nodes[i][4], tag, [(k, w[0]) for k, w in waits.items()]))
        res.append((out, cnt, (max(fin.values()), seq, fin)))
    return res


CACHE = {}


def route(core, dst, cores, topo):
    if topo.may_write(core, dst):
        return None
    c = [x for x in topo.cores_of(core) if x not in cores and topo.may_write(x, dst)]
    c = [x for x in c if topo.die(x) == topo.die(core)] or c
    return {"x": c[0], "n": c[-1]}


def rank_program(g, core, T, topo):
    cores = list(T.cores)
    rank = T.rank_of(core)

    def piece(p, buf, k, t):
        w = LH if p == "x" else 2 * LH
        return T[buf][:, k * w:k * w + (LH if t == STEPS - 1 else w)]

    def message(p, t, h, dst, out, in_):
        rid, pid = topo.addr(dst, core)
        g.remote_dma(out, in_, T.sem["a%s%d_%d" % (p, t + 1, h)], T.sem.ls, pid, rid, topo.mask(core, dst))
        return len(topo.engines(core, dst))

    def landing(p, t, h):
        return piece(p, "R%s%d" % (p.upper(), h), t + 1, t)

    def handed(p, t, h):
        return piece(p, "RY" + p.upper(), t * H + h, t)

    if rank is None:
        total = 0
        jobs = []
        for i, src in enumerate(cores):
            dst = cores[(i + 1) % N]
            ro = route(src, dst, cores, topo)
            for p in ("x", "n"):
                if ro and ro[p] == core:
                    jobs.append((p, src, dst))
        for t in range(STEPS):
            for h in range(H):
                for p, src, dst in jobs:
                    if p == "n" or t < STEPS - 1:
                        g.wait_ge(T.sem["a%s%d_%d" % (p, t + 1, h)], len(topo.engines(src, core)))
                        total += message(p, t, h, dst, landing(p, t, h), handed(p, t, h))
        if total:
            g.wait_ge(T.sem.ls, total)
        return

    if "p" not in CACHE:
        CACHE["p"] = plan()
    nxt, prv = cores[(rank + 1) % N], cores[(rank - 1) % N]
    ro_out, ro_in = route(core, nxt, cores, topo), route(prv, core, cores, topo)
    prog, cnt, _ = CACHE["p"][0 if ro_out is None else 1]
    tot = [0]

    def send(p, t, h):
        src = piece(p, "T%s%d" % (p.upper(), h), t, t)
        if ro_out is None:
            tot[0] += message(p, t, h, nxt, landing(p, t, h), src)
        else:
            tot[0] += message(p, t, h, ro_out[p], handed(p, t, h), src)

    E = {"g": g, "T": T, "send": send}
    eng = {"v": g.vector, "a": g.scalar, "t": g.tensor, "g": g, "y": g.sync}
    for rq, q, fn, tag, waits in prog:
        for key, val in waits:
            if isinstance(key, tuple):
                p, t, h = key
                frm = prv if ro_in is None else ro_in[p[1]]
                eng[rq].wait_ge(T.sem["%s%d_%d" % (p, t, h)], len(topo.engines(frm, core)))
            else:
                eng[rq].wait_ge(T.sem[CTR[key] if key in CTR else key], val)
        i = fn(E)
        if tag != "send":
            i.then_inc(T.sem[CTR[q]] if q in CTR else T.sem[tag], 1 if q in CTR else 16)
    for q in CTR:
        g.wait_ge(T.sem[CTR[q]], cnt[q])
    for n in DMAS:
        g.wait_ge(T.sem["d_" + n], 16)
    g.wait_ge(T.sem.ls, tot[0])
